import numpy as np
import ml_dtypes


def mxq(x, axis, fmt="e4m3"):
    dtype, down = {"e4m3": (ml_dtypes.float8_e4m3fn, 7), "e5m2": (ml_dtypes.float8_e5m2, 14)}[fmt]
    v = np.moveaxis(np.asarray(x, np.float32).astype(ml_dtypes.bfloat16).astype(np.float64), axis, -1)
    blocks = v.reshape(v.shape[:-1] + (-1, 32))
    amax = np.abs(blocks).max(-1, keepdims=True)
    byte = np.maximum(np.where(amax > 0, np.frexp(amax)[1] - 1 + 127, 0) - down, 1)
    scale = np.exp2(byte - 127.0)
    codes = (blocks / scale).astype(np.float32).astype(dtype).astype(np.float64)
    return np.moveaxis((codes * scale).reshape(v.shape), -1, axis)


WIDE = False


def mx_kscale(k):
    if not WIDE:
        return np.ones(k)
    levels = np.array([10, -10, 5, -5, 0])
    if k % 512:
        return np.exp2(np.random.permutation(np.resize(levels, k // 32))).repeat(32)
    a = np.empty((k // 512, 16))
    for p in range(k // 512):
        a[p, :8] = np.random.permutation(np.resize(levels, 8))
        for g in range(8):
            far = levels[np.abs(levels - a[p, g]) >= 10]
            a[p, g + 8] = far[np.random.randint(len(far))]
    return np.exp2(a.ravel()).repeat(32)


BF16 = ml_dtypes.bfloat16


def bf(x):
    return np.asarray(x, np.float32).astype(BF16)


def f64(x):
    return np.asarray(x).astype(np.float64)


E2M1 = np.array([0.0, 0.5, 1.0, 1.5, 2.0, 3.0, 4.0, 6.0, -0.0, -0.5, -1.0, -1.5, -2.0, -3.0, -4.0, -6.0])


def pack_weight(w, fmt):
    k, n = w.shape
    w = f64(bf(w)).reshape(k // 32, 32, n)
    amax = np.abs(w).max(1)
    if fmt == "e4m3":
        byte = np.frexp(amax)[1] - 1 + 127 - 7
    else:
        mant, ex = np.frexp(amax / 6.0)
        byte = np.where(mant > 0.5, ex, ex - 1) + 127
    byte = np.clip(np.where(amax > 0, byte, 1), 1, 254)
    scaled = (w * np.exp2(127.0 - byte)[:, None, :]).reshape(k, n).astype(np.float32)
    by_word = np.ascontiguousarray(scaled.reshape(k // 512, 128, 4, n).transpose(0, 1, 3, 2))
    if fmt == "e4m3":
        words = by_word.astype(ml_dtypes.float8_e4m3fn).view(np.uint8)
    else:
        c = by_word.astype(ml_dtypes.float4_e2m1fn).view(np.uint8) & 0xF
        words = c[..., 0::2] | (c[..., 1::2] << 4)
    return np.ascontiguousarray(words), np.ascontiguousarray(byte.astype(np.uint8).reshape(k // 512, 16, n))


def unpack_weight(words, scales, fmt):
    g, p, n, _ = words.shape
    if fmt == "e4m3":
        vals = np.ascontiguousarray(words).view(ml_dtypes.float8_e4m3fn).astype(np.float64)
    else:
        nib = np.empty((g, p, n, 4), np.uint8)
        nib[..., 0::2] = words & 0xF
        nib[..., 1::2] = words >> 4
        vals = E2M1[nib]
    vals = vals * np.repeat(np.exp2(scales.astype(np.float64) - 127.0), 8, axis=1)[..., None]
    return vals.transpose(0, 1, 3, 2).reshape(g * 512, n)
def pack4(w):
    words, scales = pack_weight(w, "e2m1")
    return words.reshape(words.shape[0], 128, -1), scales


def unpack4(words, scales):
    return unpack_weight(words.reshape(words.shape[0], 128, -1, 2), scales, "e2m1")


M, D, E, N, P = 1024, 1024, 512, 2048, 512


def draw0():
    u, v, w = mx_kscale(D), mx_kscale(E), mx_kscale(N)
    a = np.sqrt(0.5) / D ** 0.25
    x1 = np.random.standard_normal((M, D)) * a
    z1 = np.random.standard_normal((D, N)) * a
    hx = 0.5 * np.sum(x1 * x1, axis=1)
    hz = 0.5 * np.sum(z1 * z1, axis=0)
    x2 = np.random.standard_normal((M, E))
    z2 = np.random.standard_normal((E, N)) * 0.5 / np.sqrt(E)
    alpha = np.random.standard_normal((N, P)) / np.sqrt(N)
    z1_words, z1_scales = pack4(z1 / u[:, None])
    z2_words, z2_scales = pack4(z2 / v[:, None])
    alpha_words, alpha_scales = pack_weight(alpha / w[:, None], "e4m3")
    return {"x1": bf(x1 * u),
            "x2": bf(x2 * v),
            "z1_words": z1_words, "z1_scales": z1_scales,
            "z2_words": z2_words, "z2_scales": z2_scales,
            "alpha_words": alpha_words, "alpha_scales": alpha_scales,
            "lx": bf(hx - hx.mean()),
            "lz": bf(hz - hz.mean()),
            "amp": bf((1 + 0.1 * np.random.standard_normal(N)) * w),
            "gain": bf(1 + 0.1 * np.random.standard_normal(P)),
            "prior": bf(0.3 * np.random.standard_normal(P))}


def core(x1, x2, z1_words, z1_scales, z2_words, z2_scales, alpha_words, alpha_scales, lx, lz, amp, gain, prior):
    g1 = mxq(f64(x1), 1, "e4m3") @ unpack4(z1_words, z1_scales)
    g2 = mxq(f64(x2), 1, "e4m3") @ unpack4(z2_words, z2_scales)
    rbf = np.exp(g1 - f64(lx)[:, None] - f64(lz)[None, :])
    poly = np.square(1 + g2)
    kern = rbf * poly * f64(amp)[None, :]
    f = mxq(kern, 1, "e4m3") @ unpack_weight(alpha_words, alpha_scales, "e4m3")
    return f64(prior)[None, :] + f64(gain)[None, :] * f


def e4m3fn_bytes(y):
    return np.clip(np.asarray(y, np.float64), -448.0, 448.0).astype(np.float32).astype(ml_dtypes.float8_e4m3fn).view(np.uint8)


def e4m3fn_values(b):
    return np.asarray(b, np.uint8).view(ml_dtypes.float8_e4m3fn).astype(np.float64)


def setup_inputs():
    d = draw0()
    x0 = np.asarray(d['x1']).astype(np.float64)
    s = (np.max(np.abs(x0), axis=(0,), keepdims=True) / 448.0).astype(np.float32)
    out = {}
    for k, v in d.items():
        if k == 'x1':
            out['x1_bytes'] = e4m3fn_bytes(x0 / s.astype(np.float64))
            out['x1_scale'] = s
        else:
            out[k] = v
    return out


def reference(x1_bytes, x1_scale, x2, z1_words, z1_scales, z2_words, z2_scales, alpha_words, alpha_scales, lx, lz, amp, gain, prior):
    return core(e4m3fn_values(x1_bytes) * x1_scale.astype(np.float64), x2, z1_words, z1_scales, z2_words, z2_scales, alpha_words, alpha_scales, lx, lz, amp, gain, prior)

@@ -1,0 +1,361 @@
+from contextlib import ExitStack
+
+import concourse.mybir as mybir
+from concourse.masks import make_identity
+
+M, D, E, N, C = 1024, 1024, 512, 2048, 512
+FLOPS = 2 * M * N * (D + E) + 2 * M * N * C
+
+F32 = mybir.dt.float32
+BF16 = mybir.dt.bfloat16
+I32 = mybir.dt.int32
+U32 = mybir.dt.uint32
+U8 = mybir.dt.uint8
+FP8 = mybir.dt.float8_e4m3fn
+FP8X4 = mybir.dt.float8_e4m3fn_x4
+FP4X4 = mybir.dt.float4_e2m1fn_x4
+ALU = mybir.AluOpType
+ACT = mybir.ActivationFunctionType
+
+P = 128
+RT = M // P
+UNITS = 2 * RT
+GSET = ((0, 1), (1, 1))
+LAST_V = 1
+FIN_G = 7
+
+
+def tile_gp_product_kernel_mean_f7_kernel(
+    tc, x1_bytes, x1_scale, x2, z1_words, z1_scales, z2_words, z2_scales,
+    alpha_words, alpha_scales, lx, lz, amp, gain, prior, out,
+):
+    nc = tc.nc
+    with ExitStack() as ctx:
+        keep = ctx.enter_context(tc.tile_pool(name="keep", bufs=1))
+        work = ctx.enter_context(tc.tile_pool(name="work", bufs=3))
+        psum = ctx.enter_context(tc.psum_pool(name="psum", bufs=1))
+        ctx.enter_context(tc.manual_schedule())
+
+        amp_k = keep.tile([P, 16], BF16, name="amp_k")
+        lz_k = keep.tile([P, 16], BF16, name="lz_k")
+        lx_t = keep.tile([P, RT], BF16, name="lx_t")
+        x1q = keep.tile([P, RT, D], U8, name="x1q", align_bytes=64)
+        x2q = keep.tile([P, RT, E], BF16, name="x2q", align_bytes=64)
+        zw = keep.tile([P, 3, 2 * N], U8, name="zw", align_bytes=256)
+        zs = keep.tile([P, 3, N], U8, name="zs", align_bytes=256)
+        aw = keep.tile([P, 4, 4 * C], U8, name="aw", align_bytes=256)
+        asc = keep.tile([P, 4, C], U8, name="asc", align_bytes=256)
+        gb = keep.tile([P, C], BF16, name="gb")
+        pb = keep.tile([P, C], BF16, name="pb")
+        ident = keep.tile([P, P], F32, name="ident")
+        one = keep.tile([P, 1], F32, name="one")
+        junk = keep.tile([P, 2], F32, name="junk")
+        sb = keep.tile([P, D], F32, name="sb", align_bytes=64)
+        mant = keep.tile([P, 16], BF16, name="mant")
+        sgk = keep.tile([P, 16], BF16, name="sgk")
+        lnm = keep.tile([P, 16], F32, name="lnm")
+        lfac = keep.tile([P, 16], F32, name="lfac")
+        nlx = keep.tile([P, RT], F32, name="nlx")
+        nlxh = keep.tile([P, RT], F32, name="nlxh")
+        lb = keep.tile([P, N], F32, name="lb", align_bytes=64)
+
+        x1v = x1_bytes.rearrange("(p r) k -> p r k", r=RT)
+        x2v = x2.rearrange("(p r) k -> p r k", r=RT)
+        ov = out.rearrange("(p r) c -> p r c", r=RT)
+        z1v = z1_words.rearrange("g p n -> p g n")
+        z2v = z2_words.rearrange("g p n -> p g n")
+        awv = alpha_words.rearrange("g p n t -> p g (n t)")
+
+        nc.vector.memset(zs[:].rearrange("p g n -> p (g n)").bitcast(I32), 0)
+        nc.vector.memset(one[:], 1.0)
+        make_identity(nc, ident[:])
+        nc.gpsimd.memset(asc[:].rearrange("p g n -> p (g n)").bitcast(I32), 0)
+
+        def load_x(r0, r1):
+            nc.sync.dma_start(out=x1q[:, r0:r1, :], in_=x1v[:, r0:r1, :])
+            nc.sync.dma_start(out=x2q[:, r0:r1, :], in_=x2v[:, r0:r1, :])
+
+        def load_scales(dst, g0, src):
+            g = src.shape[0]
+            for q in range(4):
+                nc.sync.dma_start(
+                    out=dst[32 * q : 32 * q + 4, g0 : g0 + g, :].bitcast(I32),
+                    in_=src[:, 4 * q : 4 * q + 4, :].rearrange("g q n -> q g n").bitcast(I32),
+                )
+
+        def load_z(c):
+            w = slice(1024 * c, 1024 * (c + 1))
+            nc.sync.dma_start(out=zw[:, 0:2, w], in_=z1v[:, :, w])
+            nc.sync.dma_start(out=zw[:, 2:3, w], in_=z2v[:, :, w])
+
+        nc.scalar.dma_start(out=sb[:], in_=x1_scale.rearrange("o k -> (o k)").partition_broadcast(P))
+        nc.scalar.dma_start(out=amp_k[:].rearrange("p (c t) -> p c t", t=4), in_=amp.rearrange("(c p t) -> p c t", p=P, t=4))
+        nc.scalar.dma_start(out=lz_k[:].rearrange("p (c t) -> p c t", t=4), in_=lz.rearrange("(c p t) -> p c t", p=P, t=4))
+        nc.scalar.dma_start(out=lx_t[:], in_=lx.rearrange("(p r) -> p r", r=RT))
+        load_x(0, 1)
+        load_scales(zs, 0, z1_scales)
+        load_z(0)
+        load_scales(zs, 2, z2_scales)
+        load_z(1)
+        load_x(1, 2)
+        load_z(2)
+        load_z(3)
+        load_scales(asc, 0, alpha_scales)
+        nc.sync.dma_start(out=aw[:, 0:2, :], in_=awv[:, 0:2, :])
+        load_x(2, 4)
+        nc.sync.dma_start(out=aw[:, 2:4, :], in_=awv[:, 2:4, :])
+        load_x(4, 6)
+        load_x(6, 8)
+        nc.gpsimd.dma_start(out=gb[:], in_=gain.partition_broadcast(P))
+        nc.gpsimd.dma_start(out=pb[:], in_=prior.partition_broadcast(P))
+
+        tiles = {}
+
+        def on_g(n, h):
+            return n < UNITS - LAST_V and (n % 2, h) in GSET
+
+        def xw(n):
+            x1b = work.tile([P, D], BF16, name="x1b", tag="x1b", bufs=3, align_bytes=64)
+            for k in (slice(0, 512), slice(512, 1024)) if n == 0 else (slice(0, 1024),):
+                nc.vector.tensor_tensor(out=x1b[:, k], in0=x1q[:, n // 2, k].bitcast(FP8), in1=sb[:, k], op=ALU.mult)
+            tiles["x1b", n] = x1b
+
+        def xt(n):
+            w1 = tiles["x1b", n][:].bitcast(F32)
+            w2 = x2q[:, n // 2, :].bitcast(F32)
+            xa = psum.tile([P, 4, P], F32, name="xa", tag="ct", bufs=3)
+            xb = psum.tile([P, 4, P], F32, name="xb", tag="ct", bufs=3)
+            for g in range(2):
+                for u in range(2):
+                    nc.tensor.transpose(xa[:, 2 * g + u, :], w1[:, 256 * g + u : 256 * (g + 1) : 2], ident[:])
+            for u in range(2):
+                nc.tensor.transpose(xb[:, u, :], w2[:, u:256:2], ident[:])
+            tiles["xp", n] = (xa, xb)
+
+        def xv(n):
+            xg = work.tile([P, 3 * 512], BF16, name="xg", tag="xg", bufs=3, align_bytes=64)
+            xa, xb = tiles["xp", n]
+            v = xg[:].bitcast(F32).rearrange("p (g i u) -> p g i u", g=3, u=2)
+            for g in ((0, 1), (1, 2)) if n == 0 else ((0, 2),):
+                nc.scalar.copy(out=v[:, g[0] : g[1]], in_=xa[:, 2 * g[0] : 2 * g[1], :].rearrange("p (g u) i -> p g i u", u=2))
+            nc.scalar.copy(out=v[:, 2], in_=xb[:, 0:2, :].rearrange("p u i -> p i u"))
+            tiles["xg", n] = xg
+
+        def xq(n):
+            xc = work.tile([P, 3 * P], U32, name="xc", tag="xc", bufs=4, align_bytes=64)
+            xs = work.tile([P, 3 * P], U8, name="xs", tag="xs", bufs=4, align_bytes=64)
+            xg = tiles["xg", n]
+            for a, b in ((0, 1), (1, 2), (2, 3)) if n == 0 else ((0, 2), (2, 3)):
+                nc.vector.quantize_mx(
+                    out=xc[:, P * a : P * b].bitcast(FP8X4), scales=xs[:, P * a : P * b], in_=xg[:, 512 * a : 512 * b]
+                )
+            tiles["xc", n // 2] = (xc, xs)
+
+        def mm(acc, n, g, h, start, stop):
+            xc, xs = tiles["xc", n // 2]
+            c = 2 * (n % 2) + h
+            nc.tensor.matmul_mx(
+                out=acc[:],
+                lhsT=xc[:, P * g : P * (g + 1)].bitcast(FP8X4),
+                lhsT_scale=xs[:, P * g : P * (g + 1)],
+                rhs=zw[:, g, 1024 * c : 1024 * (c + 1)].bitcast(FP4X4),
+                rhs_scale=zs[:, g, 512 * c : 512 * (c + 1)],
+                start=start,
+                stop=stop,
+            )
+
+        def g1(n, h):
+            acc = psum.tile([P, 512], F32, name="g1", tag="g1", bufs=2)
+            mm(acc, n, 0, h, True, False)
+            mm(acc, n, 1, h, False, True)
+            tiles["g1", n, h] = acc
+
+        def g2(n, h):
+            acc = psum.tile([P, 512], F32, name="g2", tag="g2", bufs=2)
+            mm(acc, n, 2, h, True, True)
+            tiles["g2", n, h] = acc
+
+        def vt(n, h):
+            c = 2 * (n % 2) + h
+            t = work.tile([P, 512], F32, name="t", tag="t", bufs=6)
+            nc.vector.tensor_tensor(out=t[:], in0=tiles["g1", n, h][:], in1=lb[:, 512 * c : 512 * (c + 1)], op=ALU.subtract)
+            tiles["t", n, h] = t
+
+        def ex(n, h):
+            r = n // 2
+            e = work.tile([P, 512], F32, name="e", tag="e", bufs=8)
+            if on_g(n, h):
+                nc.scalar.activation(out=e[:], in_=tiles["t", n, h][:], func=ACT.Exp, bias=nlx[:, r : r + 1], scale=1.0)
+            else:
+                nc.scalar.activation(out=e[:], in_=tiles["t", n, h][:], func=ACT.Exp, bias=nlxh[:, r : r + 1], scale=0.5)
+            tiles["e", n, h] = e
+
+        def sq(n, h):
+            if on_g(n, h):
+                q = work.tile([P, 512], F32, name="q", tag="q", bufs=5)
+                nc.scalar.activation(out=q[:], in_=tiles["g2", n, h][:], func=ACT.Square, bias=1.0, scale=1.0)
+                tiles["q", n, h] = q
+
+        def gd(n, h):
+            if on_g(n, h):
+                cr = work.tile([P, 512], BF16, name="cr", tag="cr", bufs=8, align_bytes=64)
+                nc.gpsimd.tensor_tensor(out=cr[:], in0=tiles["e", n, h][:], in1=tiles["q", n, h][:], op=ALU.mult)
+                tiles["cr", n, h] = cr
+
+        def vy(n, h):
+            if not on_g(n, h):
+                y = work.tile([P, 512], F32, name="y", tag="y", bufs=4)
+                nc.vector.scalar_tensor_tensor(
+                    out=y[:], in0=tiles["g2", n, h][:], scalar=1.0, in1=tiles["e", n, h][:], op0=ALU.add, op1=ALU.mult
+                )
+                tiles["y", n, h] = y
+
+        def ys(n, h):
+            if not on_g(n, h):
+                cr = work.tile([P, 512], BF16, name="cr", tag="cr", bufs=8, align_bytes=64)
+                nc.scalar.activation(
+                    out=cr[:].rearrange("p (u k e) -> p u k e", u=2, e=2),
+                    in_=tiles["y", n, h][:].rearrange("p (k u e) -> p u k e", u=2, e=2),
+                    func=ACT.Square,
+                )
+                tiles["cr", n, h] = cr
+
+        def ct(n):
+            ps = psum.tile([P, 4, P], F32, name="ctc", tag="ct", bufs=3)
+            for h in range(2):
+                w = tiles["cr", n, h][:].bitcast(F32)
+                for u in range(2):
+                    if on_g(n, h):
+                        src = w[:, u:256:2]
+                    else:
+                        src = w[:, P * u : P * (u + 1)]
+                    nc.tensor.transpose(ps[:, 2 * h + u, :], src, ident[:])
+            tiles["ct", n] = ps
+
+        def cv(n, h):
+            if h == 0:
+                cg = work.tile([P, 1024], BF16, name="cg", tag="cg", bufs=4, align_bytes=64)
+                tiles["cg", n] = cg
+            c = 2 * (n % 2) + h
+            ps = tiles["ct", n][:, 2 * h : 2 * h + 2, :].bitcast(BF16)
+            nc.vector.tensor_tensor(
+                out=tiles["cg", n][:, 512 * h : 512 * (h + 1)].rearrange("p (i u e) -> p i u e", u=2, e=2),
+                in0=ps.rearrange("p u (i e) -> p i u e", e=2),
+                in1=sgk[:, 4 * c : 4 * c + 4].rearrange("p (o u e) -> p o u e", o=1, e=2).to_broadcast([P, P, 2, 2]),
+                op=ALU.mult,
+            )
+
+        def qu(n):
+            cc = work.tile([P, 256], U32, name="cc", tag="cc", bufs=4, align_bytes=64)
+            cs = work.tile([P, 256], U8, name="cs", tag="cs", bufs=4, align_bytes=64)
+            nc.vector.quantize_mx(out=cc[:].bitcast(FP8X4), scales=cs[:], in_=tiles["cg", n][:])
+            tiles["cc", n] = (cc, cs)
+
+        def pf(n):
+            r = n // 2
+            if n % 2 == 0:
+                f = psum.tile([P, C], F32, name="f", tag="f", bufs=1)
+                tiles["f", r] = f
+            cc, cs = tiles["cc", n]
+            for h in range(2):
+                j = 2 * (n % 2) + h
+                nc.tensor.matmul_mx(
+                    out=tiles["f", r][:],
+                    lhsT=cc[:, P * h : P * (h + 1)].bitcast(FP8X4),
+                    lhsT_scale=cs[:, P * h : P * (h + 1)],
+                    rhs=aw[:, j, :].bitcast(FP8X4),
+                    rhs_scale=asc[:, j, :],
+                    start=(j == 0),
+                    stop=(j == 3),
+                )
+
+        def fo(n):
+            r = n // 2
+            o1 = work.tile([P, C], F32, name="o1", tag="o1", bufs=3)
+            if r == RT - 1:
+                for k in (slice(0, 256), slice(256, 512)):
+                    nc.vector.tensor_tensor(out=o1[:, k], in0=tiles["f", r][:, k], in1=gb[:, k], op=ALU.mult)
+            elif r < FIN_G:
+                nc.scalar.copy(out=o1[:], in_=tiles["f", r][:])
+            else:
+                nc.vector.tensor_tensor(out=o1[:], in0=tiles["f", r][:], in1=gb[:], op=ALU.mult)
+            tiles["o1", r] = o1
+
+        def fp(n):
+            r = n // 2
+            o1 = tiles["o1", r]
+            o3 = work.tile([P, C], F32, name="o3", tag="o3", bufs=3)
+            if r < FIN_G:
+                o2 = work.tile([P, C], F32, name="o2", tag="o2", bufs=2)
+                nc.gpsimd.tensor_tensor(out=o2[:], in0=o1[:], in1=gb[:], op=ALU.mult)
+                nc.gpsimd.tensor_tensor(out=o3[:], in0=o2[:], in1=pb[:], op=ALU.add)
+            elif r < RT - 1:
+                nc.gpsimd.tensor_tensor(out=o3[:], in0=o1[:], in1=pb[:], op=ALU.add)
+            else:
+                for k in (slice(0, 256), slice(256, 512)):
+                    nc.vector.tensor_tensor(out=o3[:, k], in0=o1[:, k], in1=pb[:, k], op=ALU.add)
+                    nc.sync.dma_start(out=ov[:, r, k], in_=o3[:, k])
+                return
+            nc.sync.dma_start(out=ov[:, r, :], in_=o3[:])
+
+        def h_small():
+            nc.scalar.activation(out=junk[:, 0:1], in_=one[:], func=ACT.Ln)
+            nc.vector.tensor_scalar(out=mant[:].bitcast(I32), in0=amp_k[:].bitcast(I32), scalar1=0x007F007F,
+                                    scalar2=0x3F803F80, op0=ALU.bitwise_and, op1=ALU.bitwise_or)
+            nc.scalar.activation(out=lnm[:], in_=mant[:], func=ACT.Ln)
+            nc.vector.tensor_tensor(out=lfac[:], in0=lz_k[:], in1=lnm[:], op=ALU.subtract)
+            nc.scalar.activation(out=junk[:, 1:2], in_=one[:], func=ACT.Exp)
+
+        def h_lx():
+            nc.vector.tensor_scalar(out=nlx[:], in0=lx_t[:], scalar1=-1.0, scalar2=None, op0=ALU.mult)
+            nc.vector.tensor_scalar(out=nlxh[:], in0=lx_t[:], scalar1=-0.5, scalar2=None, op0=ALU.mult)
+
+        def h_l(c):
+            lp = psum.tile([P, 4, P], F32, name="lp", tag="g2", bufs=2)
+            for t in range(4):
+                k = 4 * c + t
+                nc.tensor.transpose(lp[:, t, :], lfac[:, k : k + 1].to_broadcast([P, P]), ident[:])
+            o = lb[:, 512 * c : 512 * (c + 1)].rearrange("p (k t) -> p k t", t=4)
+            i = lp[:].rearrange("p t k -> p k t")
+            if c % 2 == 0:
+                nc.vector.tensor_copy(out=o, in_=i)
+            else:
+                nc.scalar.copy(out=o, in_=i)
+
+        def h_l0():
+            h_l(0)
+
+        def h_l1():
+            h_l(1)
+
+        def h_l2():
+            h_l(2)
+
+        def h_l3():
+            h_l(3)
+
+        def h_sg():
+            nc.vector.tensor_scalar(out=sgk[:].bitcast(I32), in0=amp_k[:].bitcast(I32), scalar1=-0x007F0080,
+                                    scalar2=None, op0=ALU.bitwise_and)
+
+        def run(fn, n, h):
+            if h < 0:
+                fn(n)
+            else:
+                fn(n, h)
+
+        head = ((-1, h_l3), (-3, h_l0), (-5, h_l1), (-5, h_lx), (-6, h_small), (-1, h_sg), (-1, h_l2))
+        every = ((vt, 0, 1), (xw, -4, -1), (ys, 2, 0), (xt, -2, -1), (gd, -5, 0), (fo, 5, -1), (vy, 1, 0), (sq, 1, 1), (xv, -2, -1), (ct, 2, -1), (gd, 1, 1), (g1, -1, 0), (pf, 4, -1), (ys, 1, 1), (g1, -1, 1), (ex, 0, 0), (g2, 0, 1), (ex, 0, 1), (cv, 2, 0), (qu, 3, -1), (xq, -2, -1), (vt, -1, 0), (cv, 2, 1), (fp, 5, -1), (g2, 0, 0), (vy, 0, 1), (sq, -5, 0))
+        for s in range(-7, UNITS + 8):
+            for at, fn in head:
+                if at == s:
+                    fn()
+            for fn, lag, h in every:
+                n = s - lag
+                if n < 0 or n >= UNITS:
+                    continue
+                if fn in (xw, xt, xv, xq) and n % 2 == 1:
+                    continue
+                if fn in (fo, fp) and n % 2 == 0:
+                    continue
+                run(fn, n, h)

@@ -22,7 +22,6 @@ RT = M // P
 UNITS = 2 * RT
 GSET = ((0, 1), (1, 1))
 LAST_V = 1
-FIN_G = 7
 
 
 def tile_gp_product_kernel_mean_f7_kernel(
@@ -55,7 +54,12 @@ def tile_gp_product_kernel_mean_f7_kernel(
         sgk = keep.tile([P, 16], BF16, name="sgk")
         lnm = keep.tile([P, 16], F32, name="lnm")
         lfac = keep.tile([P, 16], F32, name="lfac")
+        s8 = keep.tile([P, 2, 4], F32, name="s8")
         nlx = keep.tile([P, RT], F32, name="nlx")
+        gmark = keep.tile([P, 1], F32, name="gmark")
+        ident_b = keep.tile([P, P], BF16, name="ident_b")
+        gk = keep.tile([P, 4], F32, name="gk")
+        pk = keep.tile([P, 4], F32, name="pk")
         nlxh = keep.tile([P, RT], F32, name="nlxh")
         lb = keep.tile([P, N], F32, name="lb", align_bytes=64)
 
@@ -88,26 +92,26 @@ def tile_gp_product_kernel_mean_f7_kernel(
             nc.sync.dma_start(out=zw[:, 0:2, w], in_=z1v[:, :, w])
             nc.sync.dma_start(out=zw[:, 2:3, w], in_=z2v[:, :, w])
 
-        nc.scalar.dma_start(out=sb[:], in_=x1_scale.rearrange("o k -> (o k)").partition_broadcast(P))
+        nc.scalar.dma_start(out=s8[:], in_=x1_scale.rearrange("o (h p c) -> p (o h) c", h=2, c=4))
         nc.scalar.dma_start(out=amp_k[:].rearrange("p (c t) -> p c t", t=4), in_=amp.rearrange("(c p t) -> p c t", p=P, t=4))
         nc.scalar.dma_start(out=lz_k[:].rearrange("p (c t) -> p c t", t=4), in_=lz.rearrange("(c p t) -> p c t", p=P, t=4))
         nc.scalar.dma_start(out=lx_t[:], in_=lx.rearrange("(p r) -> p r", r=RT))
         load_x(0, 1)
         load_scales(zs, 0, z1_scales)
-        load_z(0)
         load_scales(zs, 2, z2_scales)
+        load_scales(asc, 0, alpha_scales)
+        load_z(0)
         load_z(1)
         load_x(1, 2)
         load_z(2)
         load_z(3)
-        load_scales(asc, 0, alpha_scales)
-        nc.sync.dma_start(out=aw[:, 0:2, :], in_=awv[:, 0:2, :])
         load_x(2, 4)
+        nc.sync.dma_start(out=aw[:, 0:2, :], in_=awv[:, 0:2, :])
         nc.sync.dma_start(out=aw[:, 2:4, :], in_=awv[:, 2:4, :])
         load_x(4, 6)
         load_x(6, 8)
-        nc.gpsimd.dma_start(out=gb[:], in_=gain.partition_broadcast(P))
-        nc.gpsimd.dma_start(out=pb[:], in_=prior.partition_broadcast(P))
+        nc.sync.dma_start(out=gb[:], in_=gain.partition_broadcast(P))
+        nc.sync.dma_start(out=pb[:], in_=prior.partition_broadcast(P))
 
         tiles = {}
 
@@ -199,36 +203,36 @@ def tile_gp_product_kernel_mean_f7_kernel(
         def gd(n, h):
             if on_g(n, h):
                 cr = work.tile([P, 512], BF16, name="cr", tag="cr", bufs=8, align_bytes=64)
+                nc.gpsimd.tensor_copy(out=gmark[:], in_=tiles["t", min(n + 1, UNITS - 1), 0][:, 0:1])
                 nc.gpsimd.tensor_tensor(out=cr[:], in0=tiles["e", n, h][:], in1=tiles["q", n, h][:], op=ALU.mult)
                 tiles["cr", n, h] = cr
 
         def vy(n, h):
-            if not on_g(n, h):
-                y = work.tile([P, 512], F32, name="y", tag="y", bufs=4)
-                nc.vector.scalar_tensor_tensor(
-                    out=y[:], in0=tiles["g2", n, h][:], scalar=1.0, in1=tiles["e", n, h][:], op0=ALU.add, op1=ALU.mult
-                )
-                tiles["y", n, h] = y
+            if on_g(n, h):
+                return
+            y = work.tile([P, 512], F32, name="y", tag="y", bufs=4)
+            nc.vector.scalar_tensor_tensor(
+                out=y[:], in0=tiles["g2", n, h][:], scalar=1.0, in1=tiles["e", n, h][:], op0=ALU.add, op1=ALU.mult
+            )
+            tiles["y", n, h] = y
 
         def ys(n, h):
-            if not on_g(n, h):
-                cr = work.tile([P, 512], BF16, name="cr", tag="cr", bufs=8, align_bytes=64)
-                nc.scalar.activation(
-                    out=cr[:].rearrange("p (u k e) -> p u k e", u=2, e=2),
-                    in_=tiles["y", n, h][:].rearrange("p (k u e) -> p u k e", u=2, e=2),
-                    func=ACT.Square,
-                )
-                tiles["cr", n, h] = cr
+            if on_g(n, h):
+                return
+            cr = work.tile([P, 512], BF16, name="cr", tag="cr", bufs=8, align_bytes=64)
+            nc.scalar.activation(
+                out=cr[:].rearrange("p (u k e) -> p u k e", u=2, e=2),
+                in_=tiles["y", n, h][:].rearrange("p (k u e) -> p u k e", u=2, e=2),
+                func=ACT.Square,
+            )
+            tiles["cr", n, h] = cr
 
         def ct(n):
             ps = psum.tile([P, 4, P], F32, name="ctc", tag="ct", bufs=3)
             for h in range(2):
                 w = tiles["cr", n, h][:].bitcast(F32)
                 for u in range(2):
-                    if on_g(n, h):
-                        src = w[:, u:256:2]
-                    else:
-                        src = w[:, P * u : P * (u + 1)]
+                    src = w[:, u:256:2] if on_g(n, h) else w[:, P * u : P * (u + 1)]
                     nc.tensor.transpose(ps[:, 2 * h + u, :], src, ident[:])
             tiles["ct", n] = ps
 
@@ -253,50 +257,73 @@ def tile_gp_product_kernel_mean_f7_kernel(
 
         def pf(n):
             r = n // 2
-            if n % 2 == 0:
-                f = psum.tile([P, C], F32, name="f", tag="f", bufs=1)
+            if r == RT - 1:
+                if n % 2 == 0:
+                    f = psum.tile([P, C], F32, name="f", tag="f", bufs=1)
+                    tiles["f", r] = f
+                cc, cs = tiles["cc", n]
+                for h in range(2):
+                    j = 2 * (n % 2) + h
+                    nc.tensor.matmul_mx(
+                        out=tiles["f", r][:],
+                        lhsT=cc[:, P * h : P * (h + 1)].bitcast(FP8X4),
+                        lhsT_scale=cs[:, P * h : P * (h + 1)],
+                        rhs=aw[:, j, :].bitcast(FP8X4),
+                        rhs_scale=asc[:, j, :],
+                        start=(j == 0),
+                        stop=(j == 3),
+                    )
+            elif n % 2 == 1:
+                f = psum.tile([P, 4, P], F32, name="f", tag="f", bufs=1)
                 tiles["f", r] = f
-            cc, cs = tiles["cc", n]
-            for h in range(2):
-                j = 2 * (n % 2) + h
-                nc.tensor.matmul_mx(
-                    out=tiles["f", r][:],
-                    lhsT=cc[:, P * h : P * (h + 1)].bitcast(FP8X4),
-                    lhsT_scale=cs[:, P * h : P * (h + 1)],
-                    rhs=aw[:, j, :].bitcast(FP8X4),
-                    rhs_scale=asc[:, j, :],
-                    start=(j == 0),
-                    stop=(j == 3),
-                )
+                for q in range(4):
+                    for j in range(4):
+                        cc, cs = tiles["cc", 2 * r + j // 2]
+                        h = j % 2
+                        nc.tensor.matmul_mx(
+                            out=f[:, q, :],
+                            lhsT=aw[:, j, 512 * q : 512 * (q + 1)].bitcast(FP8X4),
+                            lhsT_scale=asc[:, j, P * q : P * (q + 1)],
+                            rhs=cc[:, P * h : P * (h + 1)].bitcast(FP8X4),
+                            rhs_scale=cs[:, P * h : P * (h + 1)],
+                            start=(j == 0),
+                            stop=(j == 3),
+                        )
 
         def fo(n):
             r = n // 2
-            o1 = work.tile([P, C], F32, name="o1", tag="o1", bufs=3)
             if r == RT - 1:
+                o1 = work.tile([P, C], F32, name="o1", tag="o1", bufs=1)
                 for k in (slice(0, 256), slice(256, 512)):
                     nc.vector.tensor_tensor(out=o1[:, k], in0=tiles["f", r][:, k], in1=gb[:, k], op=ALU.mult)
-            elif r < FIN_G:
-                nc.scalar.copy(out=o1[:], in_=tiles["f", r][:])
+                tiles["o1", r] = o1
             else:
-                nc.vector.tensor_tensor(out=o1[:], in0=tiles["f", r][:], in1=gb[:], op=ALU.mult)
-            tiles["o1", r] = o1
+                ft = work.tile([P, 4, P], F32, name="ft", tag="ft", bufs=2, align_bytes=64)
+                for q in range(4):
+                    nc.scalar.activation(
+                        out=ft[:, q, :], in_=tiles["f", r][:, q, :], func=ACT.Identity,
+                        bias=pk[:, q : q + 1], scale=gk[:, q : q + 1],
+                    )
+                tiles["ft", r] = ft
+
+        def ot(n):
+            r = n // 2
+            if r < RT - 1:
+                op = psum.tile([P, 4, P], F32, name="op", tag="ct", bufs=3)
+                for q in range(4):
+                    nc.tensor.transpose(op[:, q, :], tiles["ft", r][:, q, :], ident[:])
+                tiles["op", r] = op
 
         def fp(n):
             r = n // 2
-            o1 = tiles["o1", r]
             o3 = work.tile([P, C], F32, name="o3", tag="o3", bufs=3)
-            if r < FIN_G:
-                o2 = work.tile([P, C], F32, name="o2", tag="o2", bufs=2)
-                nc.gpsimd.tensor_tensor(out=o2[:], in0=o1[:], in1=gb[:], op=ALU.mult)
-                nc.gpsimd.tensor_tensor(out=o3[:], in0=o2[:], in1=pb[:], op=ALU.add)
-            elif r < RT - 1:
-                nc.gpsimd.tensor_tensor(out=o3[:], in0=o1[:], in1=pb[:], op=ALU.add)
+            if r < RT - 1:
+                nc.scalar.copy(out=o3[:], in_=tiles["op", r][:].rearrange("p q c -> p (q c)"))
+                nc.sync.dma_start(out=ov[:, r, :], in_=o3[:])
             else:
                 for k in (slice(0, 256), slice(256, 512)):
-                    nc.vector.tensor_tensor(out=o3[:, k], in0=o1[:, k], in1=pb[:, k], op=ALU.add)
+                    nc.vector.tensor_tensor(out=o3[:, k], in0=tiles["o1", r][:, k], in1=pb[:, k], op=ALU.add)
                     nc.sync.dma_start(out=ov[:, r, k], in_=o3[:, k])
-                return
-            nc.sync.dma_start(out=ov[:, r, :], in_=o3[:])
 
         def h_small():
             nc.scalar.activation(out=junk[:, 0:1], in_=one[:], func=ACT.Ln)
@@ -305,6 +332,27 @@ def tile_gp_product_kernel_mean_f7_kernel(
             nc.scalar.activation(out=lnm[:], in_=mant[:], func=ACT.Ln)
             nc.vector.tensor_tensor(out=lfac[:], in0=lz_k[:], in1=lnm[:], op=ALU.subtract)
             nc.scalar.activation(out=junk[:, 1:2], in_=one[:], func=ACT.Exp)
+
+        def h_sb():
+            sps = psum.tile([P, 4, P], F32, name="sps", tag="g1", bufs=2)
+            sps2 = psum.tile([P, 4, P], F32, name="sps2", tag="g1", bufs=2)
+            for h, sp in ((0, sps), (1, sps2)):
+                for c in range(4):
+                    nc.tensor.transpose(sp[:, c, :], s8[:, h, c : c + 1].to_broadcast([P, P]), ident[:])
+                o = sb[:, 512 * h : 512 * (h + 1)].rearrange("p (k c) -> p k c", c=4)
+                if h == 0:
+                    nc.vector.tensor_copy(out=o, in_=sp[:].rearrange("p c k -> p k c"))
+                else:
+                    nc.scalar.copy(out=o, in_=sp[:].rearrange("p c k -> p k c"))
+
+        def h_gp():
+            nc.vector.tensor_copy(out=ident_b[:], in_=ident[:])
+            gp = psum.tile([P, 8, P], BF16, name="gp", tag="ct", bufs=3)
+            for q in range(4):
+                nc.tensor.transpose(gp[:, q, :], gb[:, P * q : P * (q + 1)], ident_b[:])
+                nc.tensor.transpose(gp[:, 4 + q, :], pb[:, P * q : P * (q + 1)], ident_b[:])
+            nc.vector.tensor_copy(out=gk[:], in_=gp[:, 0:4, 0])
+            nc.vector.tensor_copy(out=pk[:], in_=gp[:, 4:8, 0])
 
         def h_lx():
             nc.vector.tensor_scalar(out=nlx[:], in0=lx_t[:], scalar1=-1.0, scalar2=None, op0=ALU.mult)
@@ -344,8 +392,8 @@ def tile_gp_product_kernel_mean_f7_kernel(
             else:
                 fn(n, h)
 
-        head = ((-1, h_l3), (-3, h_l0), (-5, h_l1), (-5, h_lx), (-6, h_small), (-1, h_sg), (-1, h_l2))
-        every = ((vt, 0, 1), (xw, -4, -1), (ys, 2, 0), (xt, -2, -1), (gd, -5, 0), (fo, 5, -1), (vy, 1, 0), (sq, 1, 1), (xv, -2, -1), (ct, 2, -1), (gd, 1, 1), (g1, -1, 0), (pf, 4, -1), (ys, 1, 1), (g1, -1, 1), (ex, 0, 0), (g2, 0, 1), (ex, 0, 1), (cv, 2, 0), (qu, 3, -1), (xq, -2, -1), (vt, -1, 0), (cv, 2, 1), (fp, 5, -1), (g2, 0, 0), (vy, 0, 1), (sq, -5, 0))
+        head = ((-7, h_small), (-6, h_sg), (-5, h_sb), (-4, h_l1), (-3, h_lx), (-3, h_l2), (-4, h_l3), (2, h_gp), (-3, h_l0))
+        every = ((xq, -2, -1), (qu, 3, -1), (pf, 4, -1), (xw, -4, -1), (ys, 1, 0), (ct, 2, -1), (vt, -1, 0), (sq, -1, 1), (xt, -3, -1), (xv, -3, -1), (ot, 5, -1), (g2, -1, 0), (vy, 0, 0), (fo, 4, -1), (g1, -2, 0), (gd, 1, 1), (ex, -1, 0), (ex, 0, 1), (g1, -2, 1), (vy, 1, 1), (fp, 5, -1), (cv, 2, 0), (cv, 2, 1), (ys, 1, 1), (vt, -1, 1), (g2, -2, 1))
         for s in range(-7, UNITS + 8):
             for at, fn in head:
                 if at == s:
@@ -356,6 +404,6 @@ def tile_gp_product_kernel_mean_f7_kernel(
                     continue
                 if fn in (xw, xt, xv, xq) and n % 2 == 1:
                     continue
-                if fn in (fo, fp) and n % 2 == 0:
+                if fn in (fo, ot, fp) and n % 2 == 0:
                     continue
                 run(fn, n, h)

@@ -22,6 +22,8 @@ RT = M // P
 UNITS = 2 * RT
 GSET = ((0, 1), (1, 1))
 LAST_V = 1
+NCT, NG1, NG2 = 4, 2, 2
+GPRI = (0, 1, 2, 3, 4, 5, 6)
 
 
 def tile_gp_product_kernel_mean_f7_kernel(
@@ -57,9 +59,6 @@ def tile_gp_product_kernel_mean_f7_kernel(
         s8 = keep.tile([P, 2, 4], F32, name="s8")
         nlx = keep.tile([P, RT], F32, name="nlx")
         gmark = keep.tile([P, 1], F32, name="gmark")
-        ident_b = keep.tile([P, P], BF16, name="ident_b")
-        gk = keep.tile([P, 4], F32, name="gk")
-        pk = keep.tile([P, 4], F32, name="pk")
         nlxh = keep.tile([P, RT], F32, name="nlxh")
         lb = keep.tile([P, N], F32, name="lb", align_bytes=64)
 
@@ -75,8 +74,10 @@ def tile_gp_product_kernel_mean_f7_kernel(
         make_identity(nc, ident[:])
         nc.gpsimd.memset(asc[:].rearrange("p g n -> p (g n)").bitcast(I32), 0)
 
-        def load_x(r0, r1):
+        def load_x1(r0, r1):
             nc.sync.dma_start(out=x1q[:, r0:r1, :], in_=x1v[:, r0:r1, :])
+
+        def load_x2(r0, r1):
             nc.sync.dma_start(out=x2q[:, r0:r1, :], in_=x2v[:, r0:r1, :])
 
         def load_scales(dst, g0, src):
@@ -96,22 +97,23 @@ def tile_gp_product_kernel_mean_f7_kernel(
         nc.scalar.dma_start(out=amp_k[:].rearrange("p (c t) -> p c t", t=4), in_=amp.rearrange("(c p t) -> p c t", p=P, t=4))
         nc.scalar.dma_start(out=lz_k[:].rearrange("p (c t) -> p c t", t=4), in_=lz.rearrange("(c p t) -> p c t", p=P, t=4))
         nc.scalar.dma_start(out=lx_t[:], in_=lx.rearrange("(p r) -> p r", r=RT))
-        load_x(0, 1)
+        load_x1(0, 1)
+        load_x2(0, 1)
+        load_x1(1, 4)
         load_scales(zs, 0, z1_scales)
         load_scales(zs, 2, z2_scales)
         load_scales(asc, 0, alpha_scales)
         load_z(0)
         load_z(1)
-        load_x(1, 2)
+        load_x2(1, 3)
         load_z(2)
         load_z(3)
-        load_x(2, 4)
         nc.sync.dma_start(out=aw[:, 0:2, :], in_=awv[:, 0:2, :])
-        nc.sync.dma_start(out=aw[:, 2:4, :], in_=awv[:, 2:4, :])
-        load_x(4, 6)
-        load_x(6, 8)
         nc.sync.dma_start(out=gb[:], in_=gain.partition_broadcast(P))
         nc.sync.dma_start(out=pb[:], in_=prior.partition_broadcast(P))
+        load_x1(4, 8)
+        load_x2(3, 8)
+        nc.sync.dma_start(out=aw[:, 2:4, :], in_=awv[:, 2:4, :])
 
         tiles = {}
 
@@ -119,7 +121,7 @@ def tile_gp_product_kernel_mean_f7_kernel(
             return n < UNITS - LAST_V and (n % 2, h) in GSET
 
         def xw(n):
-            x1b = work.tile([P, D], BF16, name="x1b", tag="x1b", bufs=3, align_bytes=64)
+            x1b = work.tile([P, D], BF16, name="x1b", tag="x1b", bufs=6, align_bytes=64)
             for k in (slice(0, 512), slice(512, 1024)) if n == 0 else (slice(0, 1024),):
                 nc.vector.tensor_tensor(out=x1b[:, k], in0=x1q[:, n // 2, k].bitcast(FP8), in1=sb[:, k], op=ALU.mult)
             tiles["x1b", n] = x1b
@@ -127,8 +129,8 @@ def tile_gp_product_kernel_mean_f7_kernel(
         def xt(n):
             w1 = tiles["x1b", n][:].bitcast(F32)
             w2 = x2q[:, n // 2, :].bitcast(F32)
-            xa = psum.tile([P, 4, P], F32, name="xa", tag="ct", bufs=3)
-            xb = psum.tile([P, 4, P], F32, name="xb", tag="ct", bufs=3)
+            xa = psum.tile([P, 4, P], F32, name="xa", tag="ct", bufs=NCT)
+            xb = psum.tile([P, 4, P], F32, name="xb", tag="ct", bufs=NCT)
             for g in range(2):
                 for u in range(2):
                     nc.tensor.transpose(xa[:, 2 * g + u, :], w1[:, 256 * g + u : 256 * (g + 1) : 2], ident[:])
@@ -169,13 +171,13 @@ def tile_gp_product_kernel_mean_f7_kernel(
             )
 
         def g1(n, h):
-            acc = psum.tile([P, 512], F32, name="g1", tag="g1", bufs=2)
+            acc = psum.tile([P, 512], F32, name="g1", tag="g1", bufs=NG1)
             mm(acc, n, 0, h, True, False)
             mm(acc, n, 1, h, False, True)
             tiles["g1", n, h] = acc
 
         def g2(n, h):
-            acc = psum.tile([P, 512], F32, name="g2", tag="g2", bufs=2)
+            acc = psum.tile([P, 512], F32, name="g2", tag="g2", bufs=NG2)
             mm(acc, n, 2, h, True, True)
             tiles["g2", n, h] = acc
 
@@ -227,21 +229,29 @@ def tile_gp_product_kernel_mean_f7_kernel(
             )
             tiles["cr", n, h] = cr
 
-        def ct(n):
-            ps = psum.tile([P, 4, P], F32, name="ctc", tag="ct", bufs=3)
-            for h in range(2):
-                w = tiles["cr", n, h][:].bitcast(F32)
+        def halves(n, h):
+            if n == UNITS - 1:
+                return (h,)
+            return (0, 1) if h == 1 else ()
+
+        def ct(n, h):
+            hs = halves(n, h)
+            if not hs:
+                return
+            ps = psum.tile([P, 4, P], F32, name="ctc", tag="ct", bufs=NCT)
+            for k in hs:
+                w = tiles["cr", n, k][:].bitcast(F32)
                 for u in range(2):
-                    src = w[:, u:256:2] if on_g(n, h) else w[:, P * u : P * (u + 1)]
-                    nc.tensor.transpose(ps[:, 2 * h + u, :], src, ident[:])
-            tiles["ct", n] = ps
+                    src = w[:, u:256:2] if on_g(n, k) else w[:, P * u : P * (u + 1)]
+                    nc.tensor.transpose(ps[:, 2 * k + u, :], src, ident[:])
+                tiles["ct", n, k] = ps
 
         def cv(n, h):
             if h == 0:
                 cg = work.tile([P, 1024], BF16, name="cg", tag="cg", bufs=4, align_bytes=64)
                 tiles["cg", n] = cg
             c = 2 * (n % 2) + h
-            ps = tiles["ct", n][:, 2 * h : 2 * h + 2, :].bitcast(BF16)
+            ps = tiles["ct", n, h][:, 2 * h : 2 * h + 2, :].bitcast(BF16)
             nc.vector.tensor_tensor(
                 out=tiles["cg", n][:, 512 * h : 512 * (h + 1)].rearrange("p (i u e) -> p i u e", u=2, e=2),
                 in0=ps.rearrange("p u (i e) -> p i u e", e=2),
@@ -249,46 +259,52 @@ def tile_gp_product_kernel_mean_f7_kernel(
                 op=ALU.mult,
             )
 
-        def qu(n):
-            cc = work.tile([P, 256], U32, name="cc", tag="cc", bufs=4, align_bytes=64)
-            cs = work.tile([P, 256], U8, name="cs", tag="cs", bufs=4, align_bytes=64)
-            nc.vector.quantize_mx(out=cc[:].bitcast(FP8X4), scales=cs[:], in_=tiles["cg", n][:])
-            tiles["cc", n] = (cc, cs)
+        def qu(n, h):
+            hs = halves(n, h)
+            if not hs:
+                return
+            if hs[0] == 0:
+                cc = work.tile([P, 256], U32, name="cc", tag="cc", bufs=4, align_bytes=64)
+                cs = work.tile([P, 256], U8, name="cs", tag="cs", bufs=4, align_bytes=64)
+                tiles["cc", n] = (cc, cs)
+            qc, qs = tiles["cc", n]
+            a, b = hs[0], hs[-1] + 1
+            nc.vector.quantize_mx(
+                out=qc[:, P * a : P * b].bitcast(FP8X4), scales=qs[:, P * a : P * b], in_=tiles["cg", n][:, 512 * a : 512 * b]
+            )
 
-        def pf(n):
+        def pf(n, h):
             r = n // 2
             if r == RT - 1:
-                if n % 2 == 0:
-                    f = psum.tile([P, C], F32, name="f", tag="f", bufs=1)
+                if n % 2 == 0 and h == 0:
+                    f = psum.tile([P, C], F32, name="f", tag="ct", bufs=NCT)
                     tiles["f", r] = f
                 cc, cs = tiles["cc", n]
-                for h in range(2):
-                    j = 2 * (n % 2) + h
+                j = 2 * (n % 2) + h
+                nc.tensor.matmul_mx(
+                    out=tiles["f", r][:],
+                    lhsT=cc[:, P * h : P * (h + 1)].bitcast(FP8X4),
+                    lhsT_scale=cs[:, P * h : P * (h + 1)],
+                    rhs=aw[:, j, :].bitcast(FP8X4),
+                    rhs_scale=asc[:, j, :],
+                    start=(j == 0),
+                    stop=(j == 3),
+                )
+            elif n % 2 == 1 and h == 1:
+                f = psum.tile([P, C], F32, name="f", tag="ct", bufs=NCT)
+                tiles["f", r] = f
+                for j in range(4):
+                    cc, cs = tiles["cc", 2 * r + j // 2]
+                    k = j % 2
                     nc.tensor.matmul_mx(
-                        out=tiles["f", r][:],
-                        lhsT=cc[:, P * h : P * (h + 1)].bitcast(FP8X4),
-                        lhsT_scale=cs[:, P * h : P * (h + 1)],
+                        out=f[:],
+                        lhsT=cc[:, P * k : P * (k + 1)].bitcast(FP8X4),
+                        lhsT_scale=cs[:, P * k : P * (k + 1)],
                         rhs=aw[:, j, :].bitcast(FP8X4),
                         rhs_scale=asc[:, j, :],
                         start=(j == 0),
                         stop=(j == 3),
                     )
-            elif n % 2 == 1:
-                f = psum.tile([P, 4, P], F32, name="f", tag="f", bufs=1)
-                tiles["f", r] = f
-                for q in range(4):
-                    for j in range(4):
-                        cc, cs = tiles["cc", 2 * r + j // 2]
-                        h = j % 2
-                        nc.tensor.matmul_mx(
-                            out=f[:, q, :],
-                            lhsT=aw[:, j, 512 * q : 512 * (q + 1)].bitcast(FP8X4),
-                            lhsT_scale=asc[:, j, P * q : P * (q + 1)],
-                            rhs=cc[:, P * h : P * (h + 1)].bitcast(FP8X4),
-                            rhs_scale=cs[:, P * h : P * (h + 1)],
-                            start=(j == 0),
-                            stop=(j == 3),
-                        )
 
         def fo(n):
             r = n // 2
@@ -298,27 +314,19 @@ def tile_gp_product_kernel_mean_f7_kernel(
                     nc.vector.tensor_tensor(out=o1[:, k], in0=tiles["f", r][:, k], in1=gb[:, k], op=ALU.mult)
                 tiles["o1", r] = o1
             else:
-                ft = work.tile([P, 4, P], F32, name="ft", tag="ft", bufs=2, align_bytes=64)
-                for q in range(4):
-                    nc.scalar.activation(
-                        out=ft[:, q, :], in_=tiles["f", r][:, q, :], func=ACT.Identity,
-                        bias=pk[:, q : q + 1], scale=gk[:, q : q + 1],
-                    )
-                tiles["ft", r] = ft
-
-        def ot(n):
-            r = n // 2
-            if r < RT - 1:
-                op = psum.tile([P, 4, P], F32, name="op", tag="ct", bufs=3)
-                for q in range(4):
-                    nc.tensor.transpose(op[:, q, :], tiles["ft", r][:, q, :], ident[:])
-                tiles["op", r] = op
+                o1 = work.tile([P, C], F32, name="o1d", tag="o1d", bufs=2)
+                nc.vector.tensor_tensor(out=o1[:], in0=tiles["f", r][:], in1=gb[:], op=ALU.mult)
+                tiles["o1", r] = o1
 
         def fp(n):
             r = n // 2
             o3 = work.tile([P, C], F32, name="o3", tag="o3", bufs=3)
-            if r < RT - 1:
-                nc.scalar.copy(out=o3[:], in_=tiles["op", r][:].rearrange("p q c -> p (q c)"))
+            if r in GPRI:
+                nc.gpsimd.tensor_copy(out=gmark[:], in_=tiles["t", min(n + 5, UNITS - 1), 0][:, 0:1])
+                nc.gpsimd.tensor_tensor(out=o3[:], in0=tiles["o1", r][:], in1=pb[:], op=ALU.add)
+                nc.sync.dma_start(out=ov[:, r, :], in_=o3[:])
+            elif r < RT - 1:
+                nc.vector.tensor_tensor(out=o3[:], in0=tiles["o1", r][:], in1=pb[:], op=ALU.add)
                 nc.sync.dma_start(out=ov[:, r, :], in_=o3[:])
             else:
                 for k in (slice(0, 256), slice(256, 512)):
@@ -331,11 +339,13 @@ def tile_gp_product_kernel_mean_f7_kernel(
                                     scalar2=0x3F803F80, op0=ALU.bitwise_and, op1=ALU.bitwise_or)
             nc.scalar.activation(out=lnm[:], in_=mant[:], func=ACT.Ln)
             nc.vector.tensor_tensor(out=lfac[:], in0=lz_k[:], in1=lnm[:], op=ALU.subtract)
+
+        def h_exp():
             nc.scalar.activation(out=junk[:, 1:2], in_=one[:], func=ACT.Exp)
 
         def h_sb():
-            sps = psum.tile([P, 4, P], F32, name="sps", tag="g1", bufs=2)
-            sps2 = psum.tile([P, 4, P], F32, name="sps2", tag="g1", bufs=2)
+            sps = psum.tile([P, 4, P], F32, name="sps", tag="g1", bufs=NG1)
+            sps2 = psum.tile([P, 4, P], F32, name="sps2", tag="g1", bufs=NG1)
             for h, sp in ((0, sps), (1, sps2)):
                 for c in range(4):
                     nc.tensor.transpose(sp[:, c, :], s8[:, h, c : c + 1].to_broadcast([P, P]), ident[:])
@@ -345,21 +355,12 @@ def tile_gp_product_kernel_mean_f7_kernel(
                 else:
                     nc.scalar.copy(out=o, in_=sp[:].rearrange("p c k -> p k c"))
 
-        def h_gp():
-            nc.vector.tensor_copy(out=ident_b[:], in_=ident[:])
-            gp = psum.tile([P, 8, P], BF16, name="gp", tag="ct", bufs=3)
-            for q in range(4):
-                nc.tensor.transpose(gp[:, q, :], gb[:, P * q : P * (q + 1)], ident_b[:])
-                nc.tensor.transpose(gp[:, 4 + q, :], pb[:, P * q : P * (q + 1)], ident_b[:])
-            nc.vector.tensor_copy(out=gk[:], in_=gp[:, 0:4, 0])
-            nc.vector.tensor_copy(out=pk[:], in_=gp[:, 4:8, 0])
-
         def h_lx():
             nc.vector.tensor_scalar(out=nlx[:], in0=lx_t[:], scalar1=-1.0, scalar2=None, op0=ALU.mult)
             nc.vector.tensor_scalar(out=nlxh[:], in0=lx_t[:], scalar1=-0.5, scalar2=None, op0=ALU.mult)
 
         def h_l(c):
-            lp = psum.tile([P, 4, P], F32, name="lp", tag="g2", bufs=2)
+            lp = psum.tile([P, 4, P], F32, name="lp", tag="g2", bufs=NG2)
             for t in range(4):
                 k = 4 * c + t
                 nc.tensor.transpose(lp[:, t, :], lfac[:, k : k + 1].to_broadcast([P, P]), ident[:])
@@ -392,9 +393,9 @@ def tile_gp_product_kernel_mean_f7_kernel(
             else:
                 fn(n, h)
 
-        head = ((-7, h_small), (-6, h_sg), (-5, h_sb), (-4, h_l1), (-3, h_lx), (-3, h_l2), (-4, h_l3), (2, h_gp), (-3, h_l0))
-        every = ((xq, -2, -1), (qu, 3, -1), (pf, 4, -1), (xw, -4, -1), (ys, 1, 0), (ct, 2, -1), (vt, -1, 0), (sq, -1, 1), (xt, -3, -1), (xv, -3, -1), (ot, 5, -1), (g2, -1, 0), (vy, 0, 0), (fo, 4, -1), (g1, -2, 0), (gd, 1, 1), (ex, -1, 0), (ex, 0, 1), (g1, -2, 1), (vy, 1, 1), (fp, 5, -1), (cv, 2, 0), (cv, 2, 1), (ys, 1, 1), (vt, -1, 1), (g2, -2, 1))
-        for s in range(-7, UNITS + 8):
+        head = ((-9, h_lx), (-6, h_l1), (-4, h_exp), (-12, h_small), (-3, h_l0), (-4, h_l2), (-6, h_sg), (-12, h_sb), (-2, h_l3))
+        every = ((xq, -2, -1), (ct, 3, 0), (xv, -3, -1), (gd, 1, 1), (ys, 2, 1), (g1, 0, 1), (g2, 1, 0), (pf, 4, 0), (g2, 0, 1), (fo, 5, -1), (sq, 0, 1), (fp, 5, -1), (cv, 3, 0), (g1, -1, 0), (ex, 0, 0), (vt, 0, 1), (cv, 3, 1), (pf, 4, 1), (ex, 0, 1), (vy, 1, 0), (qu, 3, 0), (xt, -4, -1), (ys, 1, 0), (vt, -1, 0), (xw, -6, -1), (ct, 2, 1), (vy, 1, 1), (qu, 3, 1))
+        for s in range(-12, UNITS + 8):
             for at, fn in head:
                 if at == s:
                     fn()
@@ -404,6 +405,6 @@ def tile_gp_product_kernel_mean_f7_kernel(
                     continue
                 if fn in (xw, xt, xv, xq) and n % 2 == 1:
                     continue
-                if fn in (fo, ot, fp) and n % 2 == 0:
+                if fn in (fo, fp) and n % 2 == 0:
                     continue
                 run(fn, n, h)

@@ -23,7 +23,7 @@ UNITS = 2 * RT
 GSET = ((0, 1), (1, 1))
 LAST_V = 1
 NCT, NG1, NG2 = 4, 2, 2
-GPRI = (0, 1, 2, 3, 4, 5, 6)
+GPRI = (0, 1, 2, 3, 4, 5)
 
 
 def tile_gp_product_kernel_mean_f7_kernel(
@@ -38,6 +38,7 @@ def tile_gp_product_kernel_mean_f7_kernel(
         ctx.enter_context(tc.manual_schedule())
 
         amp_k = keep.tile([P, 16], BF16, name="amp_k")
+        amp_r = keep.tile([P, 16], BF16, name="amp_r")
         lz_k = keep.tile([P, 16], BF16, name="lz_k")
         lx_t = keep.tile([P, RT], BF16, name="lx_t")
         x1q = keep.tile([P, RT, D], U8, name="x1q", align_bytes=64)
@@ -94,26 +95,28 @@ def tile_gp_product_kernel_mean_f7_kernel(
             nc.sync.dma_start(out=zw[:, 2:3, w], in_=z2v[:, :, w])
 
         nc.scalar.dma_start(out=s8[:], in_=x1_scale.rearrange("o (h p c) -> p (o h) c", h=2, c=4))
-        nc.scalar.dma_start(out=amp_k[:].rearrange("p (c t) -> p c t", t=4), in_=amp.rearrange("(c p t) -> p c t", p=P, t=4))
-        nc.scalar.dma_start(out=lz_k[:].rearrange("p (c t) -> p c t", t=4), in_=lz.rearrange("(c p t) -> p c t", p=P, t=4))
+        nc.scalar.dma_start(out=amp_r[:], in_=amp.rearrange("(p c) -> p c", c=16))
+        nc.scalar.dma_start(out=lz_k[:], in_=lz.rearrange("(p c) -> p c", c=16))
         nc.scalar.dma_start(out=lx_t[:], in_=lx.rearrange("(p r) -> p r", r=RT))
         load_x1(0, 1)
         load_x2(0, 1)
-        load_x1(1, 4)
+        load_x1(1, 3)
         load_scales(zs, 0, z1_scales)
         load_scales(zs, 2, z2_scales)
-        load_scales(asc, 0, alpha_scales)
         load_z(0)
+        load_x2(1, 2)
         load_z(1)
-        load_x2(1, 3)
         load_z(2)
         load_z(3)
-        nc.sync.dma_start(out=aw[:, 0:2, :], in_=awv[:, 0:2, :])
+        load_x2(2, 4)
+        nc.sync.dma_start(out=amp_k[:].rearrange("p (c t) -> p c t", t=4), in_=amp.rearrange("(c p t) -> p c t", p=P, t=4))
+        load_x1(3, 5)
+        load_scales(asc, 0, alpha_scales)
+        nc.sync.dma_start(out=aw[:], in_=awv)
+        load_x2(4, 8)
+        load_x1(5, 8)
         nc.sync.dma_start(out=gb[:], in_=gain.partition_broadcast(P))
         nc.sync.dma_start(out=pb[:], in_=prior.partition_broadcast(P))
-        load_x1(4, 8)
-        load_x2(3, 8)
-        nc.sync.dma_start(out=aw[:, 2:4, :], in_=awv[:, 2:4, :])
 
         tiles = {}
 
@@ -238,24 +241,28 @@ def tile_gp_product_kernel_mean_f7_kernel(
             hs = halves(n, h)
             if not hs:
                 return
-            ps = psum.tile([P, 4, P], F32, name="ctc", tag="ct", bufs=NCT)
+            ps = psum.tile([P, 2, 2, P], F32, name="ctc", tag="ct", bufs=NCT)
             for k in hs:
                 w = tiles["cr", n, k][:].bitcast(F32)
                 for u in range(2):
                     src = w[:, u:256:2] if on_g(n, k) else w[:, P * u : P * (u + 1)]
-                    nc.tensor.transpose(ps[:, 2 * k + u, :], src, ident[:])
+                    nc.tensor.transpose(ps[:, u, k, :], src, ident[:])
                 tiles["ct", n, k] = ps
 
         def cv(n, h):
-            if h == 0:
+            hs = halves(n, h)
+            if not hs:
+                return
+            if hs[0] == 0:
                 cg = work.tile([P, 1024], BF16, name="cg", tag="cg", bufs=4, align_bytes=64)
                 tiles["cg", n] = cg
-            c = 2 * (n % 2) + h
-            ps = tiles["ct", n, h][:, 2 * h : 2 * h + 2, :].bitcast(BF16)
+            a, b = hs[0], hs[-1] + 1
+            ps = tiles["ct", n, h][:, :, a:b, :].bitcast(BF16)
+            sg = sgk[:, 8 * (n % 2) + 4 * a : 8 * (n % 2) + 4 * b].rearrange("p (c o u e) -> p c o u e", o=1, u=2, e=2)
             nc.vector.tensor_tensor(
-                out=tiles["cg", n][:, 512 * h : 512 * (h + 1)].rearrange("p (i u e) -> p i u e", u=2, e=2),
-                in0=ps.rearrange("p u (i e) -> p i u e", e=2),
-                in1=sgk[:, 4 * c : 4 * c + 4].rearrange("p (o u e) -> p o u e", o=1, e=2).to_broadcast([P, P, 2, 2]),
+                out=tiles["cg", n][:, 512 * a : 512 * b].rearrange("p (c i u e) -> p c i u e", i=P, u=2, e=2),
+                in0=ps.rearrange("p u c (i e) -> p c i u e", e=2),
+                in1=sg.to_broadcast([P, b - a, P, 2, 2]),
                 op=ALU.mult,
             )
 
@@ -335,9 +342,11 @@ def tile_gp_product_kernel_mean_f7_kernel(
 
         def h_small():
             nc.scalar.activation(out=junk[:, 0:1], in_=one[:], func=ACT.Ln)
-            nc.vector.tensor_scalar(out=mant[:].bitcast(I32), in0=amp_k[:].bitcast(I32), scalar1=0x007F007F,
+            nc.vector.tensor_scalar(out=mant[:].bitcast(I32), in0=amp_r[:].bitcast(I32), scalar1=0x007F007F,
                                     scalar2=0x3F803F80, op0=ALU.bitwise_and, op1=ALU.bitwise_or)
             nc.scalar.activation(out=lnm[:], in_=mant[:], func=ACT.Ln)
+
+        def h_lf():
             nc.vector.tensor_tensor(out=lfac[:], in0=lz_k[:], in1=lnm[:], op=ALU.subtract)
 
         def h_exp():
@@ -364,12 +373,9 @@ def tile_gp_product_kernel_mean_f7_kernel(
             for t in range(4):
                 k = 4 * c + t
                 nc.tensor.transpose(lp[:, t, :], lfac[:, k : k + 1].to_broadcast([P, P]), ident[:])
-            o = lb[:, 512 * c : 512 * (c + 1)].rearrange("p (k t) -> p k t", t=4)
+            o = lb[:].rearrange("p (k t) -> p k t", t=16)[:, :, 4 * c : 4 * c + 4]
             i = lp[:].rearrange("p t k -> p k t")
-            if c % 2 == 0:
-                nc.vector.tensor_copy(out=o, in_=i)
-            else:
-                nc.scalar.copy(out=o, in_=i)
+            nc.scalar.copy(out=o, in_=i)
 
         def h_l0():
             h_l(0)
@@ -393,8 +399,8 @@ def tile_gp_product_kernel_mean_f7_kernel(
             else:
                 fn(n, h)
 
-        head = ((-9, h_lx), (-6, h_l1), (-4, h_exp), (-12, h_small), (-3, h_l0), (-4, h_l2), (-6, h_sg), (-12, h_sb), (-2, h_l3))
-        every = ((xq, -2, -1), (ct, 3, 0), (xv, -3, -1), (gd, 1, 1), (ys, 2, 1), (g1, 0, 1), (g2, 1, 0), (pf, 4, 0), (g2, 0, 1), (fo, 5, -1), (sq, 0, 1), (fp, 5, -1), (cv, 3, 0), (g1, -1, 0), (ex, 0, 0), (vt, 0, 1), (cv, 3, 1), (pf, 4, 1), (ex, 0, 1), (vy, 1, 0), (qu, 3, 0), (xt, -4, -1), (ys, 1, 0), (vt, -1, 0), (xw, -6, -1), (ct, 2, 1), (vy, 1, 1), (qu, 3, 1))
+        head = ((-7, h_lf), (-4, h_l0), (2, h_sg), (-2, h_l2), (-4, h_l1), (-2, h_l3), (-10, h_small), (0, h_exp), (-8, h_sb), (-5, h_lx))
+        every = ((vt, 0, 0), (ys, 3, 1), (qu, 4, 1), (pf, 5, 1), (xq, -2, -1), (fo, 5, -1), (ct, 3, 0), (g1, 0, 1), (xw, -5, -1), (cv, 3, 0), (vt, 0, 1), (xt, -3, -1), (ct, 3, 1), (g2, 1, 0), (ex, 1, 1), (sq, 1, 1), (ex, 1, 0), (xv, -3, -1), (fp, 6, -1), (cv, 3, 1), (g1, -1, 0), (gd, 1, 1), (ys, 2, 0), (vy, 1, 1), (g2, 0, 1), (vy, 1, 0), (qu, 3, 0), (pf, 4, 0))
         for s in range(-12, UNITS + 8):
             for at, fn in head:
                 if at == s:

@@ -18,12 +18,19 @@ ALU = mybir.AluOpType
 ACT = mybir.ActivationFunctionType
 
 P = 128
-RT = M // P
-UNITS = 2 * RT
-GSET = ((0, 1), (1, 1))
-LAST_V = 1
-NCT, NG1, NG2 = 4, 2, 2
-GPRI = (0, 1, 2, 3, 4, 5)
+K_GROUP = 512
+CHUNK = 512
+ROW_TILES = M // P
+UNITS = 2 * ROW_TILES
+LAST_TILE = ROW_TILES - 1
+LAST_UNIT = UNITS - 1
+
+G1_BANKS, G2_BANKS = 2, 2
+OTHER_BANKS = 4
+
+MANTISSA = 0x007F007F
+EXPONENT_OF_ONE = 0x3F803F80
+SIGN_AND_EXPONENT = -0x007F0080
 
 
 def tile_gp_product_kernel_mean_f7_kernel(
@@ -37,380 +44,420 @@ def tile_gp_product_kernel_mean_f7_kernel(
         psum = ctx.enter_context(tc.psum_pool(name="psum", bufs=1))
         ctx.enter_context(tc.manual_schedule())
 
-        amp_k = keep.tile([P, 16], BF16, name="amp_k")
-        amp_r = keep.tile([P, 16], BF16, name="amp_r")
-        lz_k = keep.tile([P, 16], BF16, name="lz_k")
-        lx_t = keep.tile([P, RT], BF16, name="lx_t")
-        x1q = keep.tile([P, RT, D], U8, name="x1q", align_bytes=64)
-        x2q = keep.tile([P, RT, E], BF16, name="x2q", align_bytes=64)
-        zw = keep.tile([P, 3, 2 * N], U8, name="zw", align_bytes=256)
-        zs = keep.tile([P, 3, N], U8, name="zs", align_bytes=256)
-        aw = keep.tile([P, 4, 4 * C], U8, name="aw", align_bytes=256)
-        asc = keep.tile([P, 4, C], U8, name="asc", align_bytes=256)
-        gb = keep.tile([P, C], BF16, name="gb")
-        pb = keep.tile([P, C], BF16, name="pb")
+        amp_words = keep.tile([P, 16], BF16, name="amp_words")
+        amp_rows = keep.tile([P, 16], BF16, name="amp_rows")
+        lz_rows = keep.tile([P, 16], BF16, name="lz_rows")
+        lx_cols = keep.tile([P, ROW_TILES], BF16, name="lx_cols")
+        x1_codes = keep.tile([P, ROW_TILES, D], U8, name="x1_codes", align_bytes=64)
+        x2_rows = keep.tile([P, ROW_TILES, E], BF16, name="x2_rows", align_bytes=64)
+        z_words = keep.tile([P, 3, 2 * N], U8, name="z_words", align_bytes=256)
+        z_planes = keep.tile([P, 3, N], U8, name="z_planes", align_bytes=256)
+        a_words = keep.tile([P, 4, 4 * C], U8, name="a_words", align_bytes=256)
+        a_planes = keep.tile([P, 4, C], U8, name="a_planes", align_bytes=256)
+        gain_all = keep.tile([P, C], BF16, name="gain_all")
+        prior_all = keep.tile([P, C], BF16, name="prior_all")
         ident = keep.tile([P, P], F32, name="ident")
         one = keep.tile([P, 1], F32, name="one")
-        junk = keep.tile([P, 2], F32, name="junk")
-        sb = keep.tile([P, D], F32, name="sb", align_bytes=64)
-        mant = keep.tile([P, 16], BF16, name="mant")
-        sgk = keep.tile([P, 16], BF16, name="sgk")
-        lnm = keep.tile([P, 16], F32, name="lnm")
-        lfac = keep.tile([P, 16], F32, name="lfac")
-        s8 = keep.tile([P, 2, 4], F32, name="s8")
-        nlx = keep.tile([P, RT], F32, name="nlx")
-        gmark = keep.tile([P, 1], F32, name="gmark")
-        nlxh = keep.tile([P, RT], F32, name="nlxh")
-        lb = keep.tile([P, N], F32, name="lb", align_bytes=64)
+        table_out = keep.tile([P, 2], F32, name="table_out")
+        scale_all = keep.tile([P, D], F32, name="scale_all", align_bytes=64)
+        mantissa = keep.tile([P, 16], BF16, name="mantissa")
+        sigma = keep.tile([P, 16], BF16, name="sigma")
+        ln_m = keep.tile([P, 16], F32, name="ln_m")
+        shift = keep.tile([P, 16], F32, name="shift")
+        scale_cols = keep.tile([P, 2, 4], F32, name="scale_cols")
+        minus_lx = keep.tile([P, ROW_TILES], F32, name="minus_lx")
+        minus_half_lx = keep.tile([P, ROW_TILES], F32, name="minus_half_lx")
+        shift_all = keep.tile([P, N], F32, name="shift_all", align_bytes=64)
 
-        x1v = x1_bytes.rearrange("(p r) k -> p r k", r=RT)
-        x2v = x2.rearrange("(p r) k -> p r k", r=RT)
-        ov = out.rearrange("(p r) c -> p r c", r=RT)
-        z1v = z1_words.rearrange("g p n -> p g n")
-        z2v = z2_words.rearrange("g p n -> p g n")
-        awv = alpha_words.rearrange("g p n t -> p g (n t)")
+        x1_view = x1_bytes.rearrange("(p r) k -> p r k", r=ROW_TILES)
+        x2_view = x2.rearrange("(p r) k -> p r k", r=ROW_TILES)
+        out_view = out.rearrange("(p r) c -> p r c", r=ROW_TILES)
+        z1_view = z1_words.rearrange("g p n -> p g n")
+        z2_view = z2_words.rearrange("g p n -> p g n")
+        a_view = alpha_words.rearrange("g p n t -> p g (n t)")
 
-        nc.vector.memset(zs[:].rearrange("p g n -> p (g n)").bitcast(I32), 0)
+        nc.vector.memset(z_planes[:].rearrange("p g n -> p (g n)").bitcast(I32), 0)
         nc.vector.memset(one[:], 1.0)
         make_identity(nc, ident[:])
-        nc.gpsimd.memset(asc[:].rearrange("p g n -> p (g n)").bitcast(I32), 0)
+        nc.gpsimd.memset(a_planes[:].rearrange("p g n -> p (g n)").bitcast(I32), 0)
 
-        def load_x1(r0, r1):
-            nc.sync.dma_start(out=x1q[:, r0:r1, :], in_=x1v[:, r0:r1, :])
+        def load_x1(first, end):
+            nc.sync.dma_start(out=x1_codes[:, first:end, :], in_=x1_view[:, first:end, :])
 
-        def load_x2(r0, r1):
-            nc.sync.dma_start(out=x2q[:, r0:r1, :], in_=x2v[:, r0:r1, :])
+        def load_x2(first, end):
+            nc.sync.dma_start(out=x2_rows[:, first:end, :], in_=x2_view[:, first:end, :])
 
-        def load_scales(dst, g0, src):
-            g = src.shape[0]
+        def load_scale_bytes(planes, first_group, source):
+            groups = source.shape[0]
             for q in range(4):
                 nc.sync.dma_start(
-                    out=dst[32 * q : 32 * q + 4, g0 : g0 + g, :].bitcast(I32),
-                    in_=src[:, 4 * q : 4 * q + 4, :].rearrange("g q n -> q g n").bitcast(I32),
+                    out=planes[32 * q : 32 * q + 4, first_group : first_group + groups, :].bitcast(I32),
+                    in_=source[:, 4 * q : 4 * q + 4, :].rearrange("g q n -> q g n").bitcast(I32),
                 )
 
-        def load_z(c):
-            w = slice(1024 * c, 1024 * (c + 1))
-            nc.sync.dma_start(out=zw[:, 0:2, w], in_=z1v[:, :, w])
-            nc.sync.dma_start(out=zw[:, 2:3, w], in_=z2v[:, :, w])
+        def load_z(chunk):
+            cols = slice(2 * CHUNK * chunk, 2 * CHUNK * (chunk + 1))
+            nc.sync.dma_start(out=z_words[:, 0:2, cols], in_=z1_view[:, :, cols])
+            nc.sync.dma_start(out=z_words[:, 2:3, cols], in_=z2_view[:, :, cols])
 
-        nc.scalar.dma_start(out=s8[:], in_=x1_scale.rearrange("o (h p c) -> p (o h) c", h=2, c=4))
-        nc.scalar.dma_start(out=amp_r[:], in_=amp.rearrange("(p c) -> p c", c=16))
-        nc.scalar.dma_start(out=lz_k[:], in_=lz.rearrange("(p c) -> p c", c=16))
-        nc.scalar.dma_start(out=lx_t[:], in_=lx.rearrange("(p r) -> p r", r=RT))
+        nc.scalar.dma_start(out=scale_cols[:], in_=x1_scale.rearrange("o (g p v) -> p (o g) v", g=2, v=4))
+        nc.scalar.dma_start(out=amp_rows[:], in_=amp.rearrange("(p v) -> p v", v=16))
+        nc.scalar.dma_start(out=lz_rows[:], in_=lz.rearrange("(p v) -> p v", v=16))
+        nc.scalar.dma_start(out=lx_cols[:], in_=lx.rearrange("(p r) -> p r", r=ROW_TILES))
         load_x1(0, 1)
         load_x2(0, 1)
         load_x1(1, 3)
-        load_scales(zs, 0, z1_scales)
-        load_scales(zs, 2, z2_scales)
+        load_scale_bytes(z_planes, 0, z1_scales)
+        load_scale_bytes(z_planes, 2, z2_scales)
         load_z(0)
         load_x2(1, 2)
         load_z(1)
         load_z(2)
         load_z(3)
         load_x2(2, 4)
-        nc.sync.dma_start(out=amp_k[:].rearrange("p (c t) -> p c t", t=4), in_=amp.rearrange("(c p t) -> p c t", p=P, t=4))
+        nc.sync.dma_start(
+            out=amp_words[:].rearrange("p (g t) -> p g t", t=4), in_=amp.rearrange("(g p t) -> p g t", p=P, t=4)
+        )
         load_x1(3, 5)
-        load_scales(asc, 0, alpha_scales)
-        nc.sync.dma_start(out=aw[:], in_=awv)
+        load_scale_bytes(a_planes, 0, alpha_scales)
+        nc.sync.dma_start(out=a_words[:], in_=a_view)
         load_x2(4, 8)
         load_x1(5, 8)
-        nc.sync.dma_start(out=gb[:], in_=gain.partition_broadcast(P))
-        nc.sync.dma_start(out=pb[:], in_=prior.partition_broadcast(P))
+        nc.sync.dma_start(out=gain_all[:], in_=gain.partition_broadcast(P))
+        nc.sync.dma_start(out=prior_all[:], in_=prior.partition_broadcast(P))
 
         tiles = {}
 
-        def on_g(n, h):
-            return n < UNITS - LAST_V and (n % 2, h) in GSET
-
-        def xw(n):
-            x1b = work.tile([P, D], BF16, name="x1b", tag="x1b", bufs=6, align_bytes=64)
+        def x_scale(n):
+            x1_rows = work.tile([P, D], BF16, name="x1_rows", tag="x1_rows", bufs=6, align_bytes=64)
             for k in (slice(0, 512), slice(512, 1024)) if n == 0 else (slice(0, 1024),):
-                nc.vector.tensor_tensor(out=x1b[:, k], in0=x1q[:, n // 2, k].bitcast(FP8), in1=sb[:, k], op=ALU.mult)
-            tiles["x1b", n] = x1b
+                nc.vector.tensor_tensor(
+                    out=x1_rows[:, k], in0=x1_codes[:, n // 2, k].bitcast(FP8), in1=scale_all[:, k], op=ALU.mult
+                )
+            tiles["x1_rows", n] = x1_rows
 
-        def xt(n):
-            w1 = tiles["x1b", n][:].bitcast(F32)
-            w2 = x2q[:, n // 2, :].bitcast(F32)
-            xa = psum.tile([P, 4, P], F32, name="xa", tag="ct", bufs=NCT)
-            xb = psum.tile([P, 4, P], F32, name="xb", tag="ct", bufs=NCT)
+        def x_turn(n):
+            x1_pairs = tiles["x1_rows", n][:].bitcast(F32)
+            x2_pairs = x2_rows[:, n // 2, :].bitcast(F32)
+            x1_turned = psum.tile([P, 4, P], F32, name="x1_turned", tag="other", bufs=OTHER_BANKS)
+            x2_turned = psum.tile([P, 4, P], F32, name="x2_turned", tag="other", bufs=OTHER_BANKS)
             for g in range(2):
                 for u in range(2):
-                    nc.tensor.transpose(xa[:, 2 * g + u, :], w1[:, 256 * g + u : 256 * (g + 1) : 2], ident[:])
+                    nc.tensor.transpose(
+                        x1_turned[:, 2 * g + u, :], x1_pairs[:, 256 * g + u : 256 * (g + 1) : 2], ident[:]
+                    )
             for u in range(2):
-                nc.tensor.transpose(xb[:, u, :], w2[:, u:256:2], ident[:])
-            tiles["xp", n] = (xa, xb)
+                nc.tensor.transpose(x2_turned[:, u, :], x2_pairs[:, u:256:2], ident[:])
+            tiles["x_turned", n] = (x1_turned, x2_turned)
 
-        def xv(n):
-            xg = work.tile([P, 3 * 512], BF16, name="xg", tag="xg", bufs=3, align_bytes=64)
-            xa, xb = tiles["xp", n]
-            v = xg[:].bitcast(F32).rearrange("p (g i u) -> p g i u", g=3, u=2)
-            for g in ((0, 1), (1, 2)) if n == 0 else ((0, 2),):
-                nc.scalar.copy(out=v[:, g[0] : g[1]], in_=xa[:, 2 * g[0] : 2 * g[1], :].rearrange("p (g u) i -> p g i u", u=2))
-            nc.scalar.copy(out=v[:, 2], in_=xb[:, 0:2, :].rearrange("p u i -> p i u"))
-            tiles["xg", n] = xg
-
-        def xq(n):
-            xc = work.tile([P, 3 * P], U32, name="xc", tag="xc", bufs=4, align_bytes=64)
-            xs = work.tile([P, 3 * P], U8, name="xs", tag="xs", bufs=4, align_bytes=64)
-            xg = tiles["xg", n]
-            for a, b in ((0, 1), (1, 2), (2, 3)) if n == 0 else ((0, 2), (2, 3)):
-                nc.vector.quantize_mx(
-                    out=xc[:, P * a : P * b].bitcast(FP8X4), scales=xs[:, P * a : P * b], in_=xg[:, 512 * a : 512 * b]
+        def x_copy(n):
+            x_grouped = work.tile([P, 3 * K_GROUP], BF16, name="x_grouped", tag="x_grouped", bufs=3, align_bytes=64)
+            x1_turned, x2_turned = tiles["x_turned", n]
+            pairs = x_grouped[:].bitcast(F32).rearrange("p (g i u) -> p g i u", g=3, u=2)
+            for first, end in ((0, 1), (1, 2)) if n == 0 else ((0, 2),):
+                nc.scalar.copy(
+                    out=pairs[:, first:end],
+                    in_=x1_turned[:, 2 * first : 2 * end, :].rearrange("p (g u) i -> p g i u", u=2),
                 )
-            tiles["xc", n // 2] = (xc, xs)
+            nc.scalar.copy(out=pairs[:, 2], in_=x2_turned[:, 0:2, :].rearrange("p u i -> p i u"))
+            tiles["x_grouped", n] = x_grouped
 
-        def mm(acc, n, g, h, start, stop):
-            xc, xs = tiles["xc", n // 2]
-            c = 2 * (n % 2) + h
+        def x_quant(n):
+            x_words = work.tile([P, 3 * P], U32, name="x_words", tag="x_words", bufs=4, align_bytes=64)
+            x_planes = work.tile([P, 3 * P], U8, name="x_planes", tag="x_planes", bufs=4, align_bytes=64)
+            for first, end in ((0, 1), (1, 2), (2, 3)) if n == 0 else ((0, 2), (2, 3)):
+                nc.vector.quantize_mx(
+                    out=x_words[:, P * first : P * end].bitcast(FP8X4),
+                    scales=x_planes[:, P * first : P * end],
+                    in_=tiles["x_grouped", n][:, K_GROUP * first : K_GROUP * end],
+                )
+            tiles["x_mx", n // 2] = (x_words, x_planes)
+
+        def x_times_z(acc, n, g, h, start, stop):
+            x_words, x_planes = tiles["x_mx", n // 2]
+            chunk = 2 * (n % 2) + h
             nc.tensor.matmul_mx(
                 out=acc[:],
-                lhsT=xc[:, P * g : P * (g + 1)].bitcast(FP8X4),
-                lhsT_scale=xs[:, P * g : P * (g + 1)],
-                rhs=zw[:, g, 1024 * c : 1024 * (c + 1)].bitcast(FP4X4),
-                rhs_scale=zs[:, g, 512 * c : 512 * (c + 1)],
+                lhsT=x_words[:, P * g : P * (g + 1)].bitcast(FP8X4),
+                lhsT_scale=x_planes[:, P * g : P * (g + 1)],
+                rhs=z_words[:, g, 2 * CHUNK * chunk : 2 * CHUNK * (chunk + 1)].bitcast(FP4X4),
+                rhs_scale=z_planes[:, g, CHUNK * chunk : CHUNK * (chunk + 1)],
                 start=start,
                 stop=stop,
             )
 
-        def g1(n, h):
-            acc = psum.tile([P, 512], F32, name="g1", tag="g1", bufs=NG1)
-            mm(acc, n, 0, h, True, False)
-            mm(acc, n, 1, h, False, True)
+        def g1_mm(n, h):
+            acc = psum.tile([P, CHUNK], F32, name="g1", tag="g1", bufs=G1_BANKS)
+            x_times_z(acc, n, 0, h, True, False)
+            x_times_z(acc, n, 1, h, False, True)
             tiles["g1", n, h] = acc
 
-        def g2(n, h):
-            acc = psum.tile([P, 512], F32, name="g2", tag="g2", bufs=NG2)
-            mm(acc, n, 2, h, True, True)
+        def g2_mm(n, h):
+            acc = psum.tile([P, CHUNK], F32, name="g2", tag="g2", bufs=G2_BANKS)
+            x_times_z(acc, n, 2, h, True, True)
             tiles["g2", n, h] = acc
 
-        def vt(n, h):
-            c = 2 * (n % 2) + h
-            t = work.tile([P, 512], F32, name="t", tag="t", bufs=6)
-            nc.vector.tensor_tensor(out=t[:], in0=tiles["g1", n, h][:], in1=lb[:, 512 * c : 512 * (c + 1)], op=ALU.subtract)
+        def on_gpsimd(n, h):
+            return h == 1 and n < LAST_UNIT
+
+        def exponent(n, h):
+            chunk = 2 * (n % 2) + h
+            t = work.tile([P, CHUNK], F32, name="t", tag="t", bufs=6)
+            nc.vector.tensor_tensor(
+                out=t[:], in0=tiles["g1", n, h][:], in1=shift_all[:, CHUNK * chunk : CHUNK * (chunk + 1)], op=ALU.subtract
+            )
             tiles["t", n, h] = t
 
-        def ex(n, h):
+        def exponential(n, h):
             r = n // 2
-            e = work.tile([P, 512], F32, name="e", tag="e", bufs=8)
-            if on_g(n, h):
-                nc.scalar.activation(out=e[:], in_=tiles["t", n, h][:], func=ACT.Exp, bias=nlx[:, r : r + 1], scale=1.0)
+            e = work.tile([P, CHUNK], F32, name="e", tag="e", bufs=8)
+            if on_gpsimd(n, h):
+                nc.scalar.activation(
+                    out=e[:], in_=tiles["t", n, h][:], func=ACT.Exp, bias=minus_lx[:, r : r + 1], scale=1.0
+                )
             else:
-                nc.scalar.activation(out=e[:], in_=tiles["t", n, h][:], func=ACT.Exp, bias=nlxh[:, r : r + 1], scale=0.5)
+                nc.scalar.activation(
+                    out=e[:], in_=tiles["t", n, h][:], func=ACT.Exp, bias=minus_half_lx[:, r : r + 1], scale=0.5
+                )
             tiles["e", n, h] = e
 
-        def sq(n, h):
-            if on_g(n, h):
-                q = work.tile([P, 512], F32, name="q", tag="q", bufs=5)
+        def poly_square(n, h):
+            if on_gpsimd(n, h):
+                q = work.tile([P, CHUNK], F32, name="q", tag="q", bufs=5)
                 nc.scalar.activation(out=q[:], in_=tiles["g2", n, h][:], func=ACT.Square, bias=1.0, scale=1.0)
                 tiles["q", n, h] = q
 
-        def gd(n, h):
-            if on_g(n, h):
-                cr = work.tile([P, 512], BF16, name="cr", tag="cr", bufs=8, align_bytes=64)
-                nc.gpsimd.tensor_copy(out=gmark[:], in_=tiles["t", min(n + 1, UNITS - 1), 0][:, 0:1])
-                nc.gpsimd.tensor_tensor(out=cr[:], in0=tiles["e", n, h][:], in1=tiles["q", n, h][:], op=ALU.mult)
-                tiles["cr", n, h] = cr
+        def gpsimd_product(n, h):
+            if on_gpsimd(n, h):
+                c_rows = work.tile([P, CHUNK], BF16, name="c_rows", tag="c_rows", bufs=8, align_bytes=64)
+                nc.gpsimd.tensor_tensor(out=c_rows[:], in0=tiles["e", n, h][:], in1=tiles["q", n, h][:], op=ALU.mult)
+                tiles["c_rows", n, h] = c_rows
 
-        def vy(n, h):
-            if on_g(n, h):
-                return
-            y = work.tile([P, 512], F32, name="y", tag="y", bufs=4)
-            nc.vector.scalar_tensor_tensor(
-                out=y[:], in0=tiles["g2", n, h][:], scalar=1.0, in1=tiles["e", n, h][:], op0=ALU.add, op1=ALU.mult
-            )
-            tiles["y", n, h] = y
+        def root_product(n, h):
+            if not on_gpsimd(n, h):
+                y = work.tile([P, CHUNK], F32, name="y", tag="y", bufs=4)
+                nc.vector.scalar_tensor_tensor(
+                    out=y[:], in0=tiles["g2", n, h][:], scalar=1.0, in1=tiles["e", n, h][:], op0=ALU.add, op1=ALU.mult
+                )
+                tiles["y", n, h] = y
 
-        def ys(n, h):
-            if on_g(n, h):
-                return
-            cr = work.tile([P, 512], BF16, name="cr", tag="cr", bufs=8, align_bytes=64)
-            nc.scalar.activation(
-                out=cr[:].rearrange("p (u k e) -> p u k e", u=2, e=2),
-                in_=tiles["y", n, h][:].rearrange("p (k u e) -> p u k e", u=2, e=2),
-                func=ACT.Square,
-            )
-            tiles["cr", n, h] = cr
+        def root_square(n, h):
+            if not on_gpsimd(n, h):
+                c_rows = work.tile([P, CHUNK], BF16, name="c_rows", tag="c_rows", bufs=8, align_bytes=64)
+                nc.scalar.activation(
+                    out=c_rows[:].rearrange("i (u p e) -> i u p e", u=2, e=2),
+                    in_=tiles["y", n, h][:].rearrange("i (p u e) -> i u p e", u=2, e=2),
+                    func=ACT.Square,
+                )
+                tiles["c_rows", n, h] = c_rows
 
-        def halves(n, h):
-            if n == UNITS - 1:
+        def chunks_now(n, h):
+            if n == LAST_UNIT:
                 return (h,)
             return (0, 1) if h == 1 else ()
 
-        def ct(n, h):
-            hs = halves(n, h)
-            if not hs:
+        def c_turn(n, h):
+            chunks = chunks_now(n, h)
+            if not chunks:
                 return
-            ps = psum.tile([P, 2, 2, P], F32, name="ctc", tag="ct", bufs=NCT)
-            for k in hs:
-                w = tiles["cr", n, k][:].bitcast(F32)
+            turned = psum.tile([P, 2, 2, P], F32, name="c_turned", tag="other", bufs=OTHER_BANKS)
+            for k in chunks:
+                pairs = tiles["c_rows", n, k][:].bitcast(F32)
                 for u in range(2):
-                    src = w[:, u:256:2] if on_g(n, k) else w[:, P * u : P * (u + 1)]
-                    nc.tensor.transpose(ps[:, u, k, :], src, ident[:])
-                tiles["ct", n, k] = ps
+                    words = pairs[:, u:256:2] if on_gpsimd(n, k) else pairs[:, P * u : P * (u + 1)]
+                    nc.tensor.transpose(turned[:, u, k, :], words, ident[:])
+                tiles["c_turned", n, k] = turned
 
-        def cv(n, h):
-            hs = halves(n, h)
-            if not hs:
+        def c_copy(n, h):
+            chunks = chunks_now(n, h)
+            if not chunks:
                 return
-            if hs[0] == 0:
-                cg = work.tile([P, 1024], BF16, name="cg", tag="cg", bufs=4, align_bytes=64)
-                tiles["cg", n] = cg
-            a, b = hs[0], hs[-1] + 1
-            ps = tiles["ct", n, h][:, :, a:b, :].bitcast(BF16)
-            sg = sgk[:, 8 * (n % 2) + 4 * a : 8 * (n % 2) + 4 * b].rearrange("p (c o u e) -> p c o u e", o=1, u=2, e=2)
+            if chunks[0] == 0:
+                grouped = work.tile([P, 2 * CHUNK], BF16, name="c_grouped", tag="c_grouped", bufs=4, align_bytes=64)
+                tiles["c_grouped", n] = grouped
+            first, end = chunks[0], chunks[-1] + 1
+            turned = tiles["c_turned", n, h][:, :, first:end, :].bitcast(BF16)
+            sigma_cols = sigma[:, 8 * (n % 2) + 4 * first : 8 * (n % 2) + 4 * end].rearrange(
+                "p (c o u e) -> p c o u e", o=1, u=2, e=2
+            )
             nc.vector.tensor_tensor(
-                out=tiles["cg", n][:, 512 * a : 512 * b].rearrange("p (c i u e) -> p c i u e", i=P, u=2, e=2),
-                in0=ps.rearrange("p u c (i e) -> p c i u e", e=2),
-                in1=sg.to_broadcast([P, b - a, P, 2, 2]),
+                out=tiles["c_grouped", n][:, CHUNK * first : CHUNK * end].rearrange(
+                    "p (c i u e) -> p c i u e", i=P, u=2, e=2
+                ),
+                in0=turned.rearrange("p u c (i e) -> p c i u e", e=2),
+                in1=sigma_cols.to_broadcast([P, end - first, P, 2, 2]),
                 op=ALU.mult,
             )
 
-        def qu(n, h):
-            hs = halves(n, h)
-            if not hs:
+        def c_quant(n, h):
+            chunks = chunks_now(n, h)
+            if not chunks:
                 return
-            if hs[0] == 0:
-                cc = work.tile([P, 256], U32, name="cc", tag="cc", bufs=4, align_bytes=64)
-                cs = work.tile([P, 256], U8, name="cs", tag="cs", bufs=4, align_bytes=64)
-                tiles["cc", n] = (cc, cs)
-            qc, qs = tiles["cc", n]
-            a, b = hs[0], hs[-1] + 1
+            if chunks[0] == 0:
+                words = work.tile([P, 2 * P], U32, name="c_words", tag="c_words", bufs=4, align_bytes=64)
+                planes = work.tile([P, 2 * P], U8, name="c_planes", tag="c_planes", bufs=4, align_bytes=64)
+                tiles["c_mx", n] = (words, planes)
+            c_words, c_planes = tiles["c_mx", n]
+            first, end = chunks[0], chunks[-1] + 1
             nc.vector.quantize_mx(
-                out=qc[:, P * a : P * b].bitcast(FP8X4), scales=qs[:, P * a : P * b], in_=tiles["cg", n][:, 512 * a : 512 * b]
+                out=c_words[:, P * first : P * end].bitcast(FP8X4),
+                scales=c_planes[:, P * first : P * end],
+                in_=tiles["c_grouped", n][:, CHUNK * first : CHUNK * end],
             )
 
-        def pf(n, h):
-            r = n // 2
-            if r == RT - 1:
-                if n % 2 == 0 and h == 0:
-                    f = psum.tile([P, C], F32, name="f", tag="ct", bufs=NCT)
-                    tiles["f", r] = f
-                cc, cs = tiles["cc", n]
-                j = 2 * (n % 2) + h
-                nc.tensor.matmul_mx(
-                    out=tiles["f", r][:],
-                    lhsT=cc[:, P * h : P * (h + 1)].bitcast(FP8X4),
-                    lhsT_scale=cs[:, P * h : P * (h + 1)],
-                    rhs=aw[:, j, :].bitcast(FP8X4),
-                    rhs_scale=asc[:, j, :],
-                    start=(j == 0),
-                    stop=(j == 3),
-                )
-            elif n % 2 == 1 and h == 1:
-                f = psum.tile([P, C], F32, name="f", tag="ct", bufs=NCT)
-                tiles["f", r] = f
-                for j in range(4):
-                    cc, cs = tiles["cc", 2 * r + j // 2]
-                    k = j % 2
-                    nc.tensor.matmul_mx(
-                        out=f[:],
-                        lhsT=cc[:, P * k : P * (k + 1)].bitcast(FP8X4),
-                        lhsT_scale=cs[:, P * k : P * (k + 1)],
-                        rhs=aw[:, j, :].bitcast(FP8X4),
-                        rhs_scale=asc[:, j, :],
-                        start=(j == 0),
-                        stop=(j == 3),
-                    )
+        def c_times_a(acc, r, chunk):
+            c_words, c_planes = tiles["c_mx", 2 * r + chunk // 2]
+            cols = slice(P * (chunk % 2), P * (chunk % 2 + 1))
+            nc.tensor.matmul_mx(
+                out=acc[:],
+                lhsT=c_words[:, cols].bitcast(FP8X4),
+                lhsT_scale=c_planes[:, cols],
+                rhs=a_words[:, chunk, :].bitcast(FP8X4),
+                rhs_scale=a_planes[:, chunk, :],
+                start=(chunk == 0),
+                stop=(chunk == 3),
+            )
 
-        def fo(n):
+        def f_mm(n, h):
             r = n // 2
-            if r == RT - 1:
-                o1 = work.tile([P, C], F32, name="o1", tag="o1", bufs=1)
-                for k in (slice(0, 256), slice(256, 512)):
-                    nc.vector.tensor_tensor(out=o1[:, k], in0=tiles["f", r][:, k], in1=gb[:, k], op=ALU.mult)
-                tiles["o1", r] = o1
+            chunk = 2 * (n % 2) + h
+            passes = (chunk,) if r == LAST_TILE else range(4) if chunk == 3 else ()
+            for c in passes:
+                if c == 0:
+                    acc = psum.tile([P, C], F32, name="f", tag="other", bufs=OTHER_BANKS)
+                    tiles["f", r] = acc
+                c_times_a(tiles["f", r], r, c)
+
+        output_halves = (slice(0, C // 2), slice(C // 2, C))
+
+        def f_gain(n):
+            r = n // 2
+            if r == LAST_TILE:
+                scaled = work.tile([P, C], F32, name="scaled_last", tag="scaled_last", bufs=1)
+                for c in output_halves:
+                    nc.vector.tensor_tensor(out=scaled[:, c], in0=tiles["f", r][:, c], in1=gain_all[:, c], op=ALU.mult)
             else:
-                o1 = work.tile([P, C], F32, name="o1d", tag="o1d", bufs=2)
-                nc.vector.tensor_tensor(out=o1[:], in0=tiles["f", r][:], in1=gb[:], op=ALU.mult)
-                tiles["o1", r] = o1
+                scaled = work.tile([P, C], F32, name="scaled", tag="scaled", bufs=2)
+                nc.vector.tensor_tensor(out=scaled[:], in0=tiles["f", r][:], in1=gain_all[:], op=ALU.mult)
+            tiles["scaled", r] = scaled
 
-        def fp(n):
+        def f_prior(n):
             r = n // 2
-            o3 = work.tile([P, C], F32, name="o3", tag="o3", bufs=3)
-            if r in GPRI:
-                nc.gpsimd.tensor_copy(out=gmark[:], in_=tiles["t", min(n + 5, UNITS - 1), 0][:, 0:1])
-                nc.gpsimd.tensor_tensor(out=o3[:], in0=tiles["o1", r][:], in1=pb[:], op=ALU.add)
-                nc.sync.dma_start(out=ov[:, r, :], in_=o3[:])
-            elif r < RT - 1:
-                nc.vector.tensor_tensor(out=o3[:], in0=tiles["o1", r][:], in1=pb[:], op=ALU.add)
-                nc.sync.dma_start(out=ov[:, r, :], in_=o3[:])
+            mean = work.tile([P, C], F32, name="mean", tag="mean", bufs=3)
+            scaled = tiles["scaled", r]
+            if r < LAST_TILE - 1:
+                nc.gpsimd.tensor_tensor(out=mean[:], in0=scaled[:], in1=prior_all[:], op=ALU.add)
+                nc.sync.dma_start(out=out_view[:, r, :], in_=mean[:])
+            elif r < LAST_TILE:
+                nc.vector.tensor_tensor(out=mean[:], in0=scaled[:], in1=prior_all[:], op=ALU.add)
+                nc.sync.dma_start(out=out_view[:, r, :], in_=mean[:])
             else:
-                for k in (slice(0, 256), slice(256, 512)):
-                    nc.vector.tensor_tensor(out=o3[:, k], in0=tiles["o1", r][:, k], in1=pb[:, k], op=ALU.add)
-                    nc.sync.dma_start(out=ov[:, r, k], in_=o3[:, k])
+                for c in output_halves:
+                    nc.vector.tensor_tensor(out=mean[:, c], in0=scaled[:, c], in1=prior_all[:, c], op=ALU.add)
+                    nc.sync.dma_start(out=out_view[:, r, c], in_=mean[:, c])
 
-        def h_small():
-            nc.scalar.activation(out=junk[:, 0:1], in_=one[:], func=ACT.Ln)
-            nc.vector.tensor_scalar(out=mant[:].bitcast(I32), in0=amp_r[:].bitcast(I32), scalar1=0x007F007F,
-                                    scalar2=0x3F803F80, op0=ALU.bitwise_and, op1=ALU.bitwise_or)
-            nc.scalar.activation(out=lnm[:], in_=mant[:], func=ACT.Ln)
+        def make_ln():
+            nc.scalar.activation(out=table_out[:, 0:1], in_=one[:], func=ACT.Ln)
+            nc.vector.tensor_scalar(
+                out=mantissa[:].bitcast(I32), in0=amp_rows[:].bitcast(I32), scalar1=MANTISSA,
+                scalar2=EXPONENT_OF_ONE, op0=ALU.bitwise_and, op1=ALU.bitwise_or,
+            )
+            nc.scalar.activation(out=ln_m[:], in_=mantissa[:], func=ACT.Ln)
 
-        def h_lf():
-            nc.vector.tensor_tensor(out=lfac[:], in0=lz_k[:], in1=lnm[:], op=ALU.subtract)
+        def make_shift():
+            nc.vector.tensor_tensor(out=shift[:], in0=lz_rows[:], in1=ln_m[:], op=ALU.subtract)
 
-        def h_exp():
-            nc.scalar.activation(out=junk[:, 1:2], in_=one[:], func=ACT.Exp)
+        def load_exp_table():
+            nc.scalar.activation(out=table_out[:, 1:2], in_=one[:], func=ACT.Exp)
 
-        def h_sb():
-            sps = psum.tile([P, 4, P], F32, name="sps", tag="g1", bufs=NG1)
-            sps2 = psum.tile([P, 4, P], F32, name="sps2", tag="g1", bufs=NG1)
-            for h, sp in ((0, sps), (1, sps2)):
-                for c in range(4):
-                    nc.tensor.transpose(sp[:, c, :], s8[:, h, c : c + 1].to_broadcast([P, P]), ident[:])
-                o = sb[:, 512 * h : 512 * (h + 1)].rearrange("p (k c) -> p k c", c=4)
-                if h == 0:
-                    nc.vector.tensor_copy(out=o, in_=sp[:].rearrange("p c k -> p k c"))
+        def spread_scale():
+            banks = []
+            for g in range(2):
+                spread = psum.tile([P, 4, P], F32, name="scale_spread", tag="g1", bufs=G1_BANKS)
+                banks.append(spread)
+            for g in range(2):
+                for v in range(4):
+                    nc.tensor.transpose(banks[g][:, v, :], scale_cols[:, g, v : v + 1].to_broadcast([P, P]), ident[:])
+                cols = scale_all[:, K_GROUP * g : K_GROUP * (g + 1)].rearrange("i (p v) -> i p v", v=4)
+                if g == 0:
+                    nc.vector.tensor_copy(out=cols, in_=banks[g][:].rearrange("i v p -> i p v"))
                 else:
-                    nc.scalar.copy(out=o, in_=sp[:].rearrange("p c k -> p k c"))
+                    nc.scalar.copy(out=cols, in_=banks[g][:].rearrange("i v p -> i p v"))
 
-        def h_lx():
-            nc.vector.tensor_scalar(out=nlx[:], in0=lx_t[:], scalar1=-1.0, scalar2=None, op0=ALU.mult)
-            nc.vector.tensor_scalar(out=nlxh[:], in0=lx_t[:], scalar1=-0.5, scalar2=None, op0=ALU.mult)
+        def make_lx():
+            nc.vector.tensor_scalar(out=minus_lx[:], in0=lx_cols[:], scalar1=-1.0, scalar2=None, op0=ALU.mult)
+            nc.vector.tensor_scalar(out=minus_half_lx[:], in0=lx_cols[:], scalar1=-0.5, scalar2=None, op0=ALU.mult)
 
-        def h_l(c):
-            lp = psum.tile([P, 4, P], F32, name="lp", tag="g2", bufs=NG2)
-            for t in range(4):
-                k = 4 * c + t
-                nc.tensor.transpose(lp[:, t, :], lfac[:, k : k + 1].to_broadcast([P, P]), ident[:])
-            o = lb[:].rearrange("p (k t) -> p k t", t=16)[:, :, 4 * c : 4 * c + 4]
-            i = lp[:].rearrange("p t k -> p k t")
-            nc.scalar.copy(out=o, in_=i)
+        def spread_shift(quarter):
+            spread = psum.tile([P, 4, P], F32, name="shift_spread", tag="g2", bufs=G2_BANKS)
+            for k in range(4):
+                v = 4 * quarter + k
+                nc.tensor.transpose(spread[:, k, :], shift[:, v : v + 1].to_broadcast([P, P]), ident[:])
+            nc.scalar.copy(
+                out=shift_all[:].rearrange("i (p v) -> i p v", v=16)[:, :, 4 * quarter : 4 * quarter + 4],
+                in_=spread[:].rearrange("i k p -> i p k"),
+            )
 
-        def h_l0():
-            h_l(0)
+        def make_sigma():
+            nc.vector.tensor_scalar(
+                out=sigma[:].bitcast(I32), in0=amp_words[:].bitcast(I32), scalar1=SIGN_AND_EXPONENT,
+                scalar2=None, op0=ALU.bitwise_and,
+            )
 
-        def h_l1():
-            h_l(1)
+        stages = (
+            (c_turn, 3, 0),
+            (g1_mm, 0, 1),
+            (c_quant, 4, 0),
+            (c_turn, 3, 1),
+            (root_product, 2, 0),
+            (x_quant, -2, None),
+            (c_quant, 4, 1),
+            (exponential, 1, 1),
+            (root_square, 2, 1),
+            (x_scale, -5, None),
+            (f_gain, 5, None),
+            (gpsimd_product, 2, 1),
+            (x_turn, -3, None),
+            (f_prior, 6, None),
+            (poly_square, 1, 1),
+            (exponent, 0, 1),
+            (g1_mm, -1, 0),
+            (exponential, 1, 0),
+            (g2_mm, 1, 0),
+            (c_copy, 3, 0),
+            (root_product, 1, 1),
+            (f_mm, 4, 0),
+            (root_square, 2, 0),
+            (g2_mm, 0, 1),
+            (f_mm, 4, 1),
+            (c_copy, 3, 1),
+            (exponent, -1, 0),
+            (x_copy, -3, None),
+        )
+        x_stages = (x_scale, x_turn, x_copy, x_quant)
+        f_stages = (f_gain, f_prior)
 
-        def h_l2():
-            h_l(2)
+        constants = {
+            -9: (make_ln,),
+            -8: (spread_scale, make_shift, lambda: spread_shift(0)),
+            -7: (make_lx,),
+            -6: (lambda: spread_shift(1),),
+            -2: (lambda: spread_shift(2),),
+            -1: (lambda: spread_shift(3),),
+            0: (load_exp_table,),
+            1: (make_sigma,),
+        }
 
-        def h_l3():
-            h_l(3)
-
-        def h_sg():
-            nc.vector.tensor_scalar(out=sgk[:].bitcast(I32), in0=amp_k[:].bitcast(I32), scalar1=-0x007F0080,
-                                    scalar2=None, op0=ALU.bitwise_and)
-
-        def run(fn, n, h):
-            if h < 0:
-                fn(n)
-            else:
-                fn(n, h)
-
-        head = ((-7, h_lf), (-4, h_l0), (2, h_sg), (-2, h_l2), (-4, h_l1), (-2, h_l3), (-10, h_small), (0, h_exp), (-8, h_sb), (-5, h_lx))
-        every = ((vt, 0, 0), (ys, 3, 1), (qu, 4, 1), (pf, 5, 1), (xq, -2, -1), (fo, 5, -1), (ct, 3, 0), (g1, 0, 1), (xw, -5, -1), (cv, 3, 0), (vt, 0, 1), (xt, -3, -1), (ct, 3, 1), (g2, 1, 0), (ex, 1, 1), (sq, 1, 1), (ex, 1, 0), (xv, -3, -1), (fp, 6, -1), (cv, 3, 1), (g1, -1, 0), (gd, 1, 1), (ys, 2, 0), (vy, 1, 1), (g2, 0, 1), (vy, 1, 0), (qu, 3, 0), (pf, 4, 0))
-        for s in range(-12, UNITS + 8):
-            for at, fn in head:
-                if at == s:
-                    fn()
-            for fn, lag, h in every:
+        first_step = min(constants)
+        last_step = LAST_UNIT + max([lag for stage, lag, h in stages])
+        for s in range(first_step, last_step + 1):
+            for make in constants.get(s, ()):
+                make()
+            for stage, lag, h in stages:
                 n = s - lag
-                if n < 0 or n >= UNITS:
+                if not 0 <= n <= LAST_UNIT:
                     continue
-                if fn in (xw, xt, xv, xq) and n % 2 == 1:
-                    continue
-                if fn in (fo, fp) and n % 2 == 0:
-                    continue
-                run(fn, n, h)
+                if h is not None:
+                    stage(n, h)
+                elif (stage in x_stages and n % 2 == 0) or (stage in f_stages and n % 2 == 1):
+                    stage(n)

from contextlib import ExitStack

import concourse.mybir as mybir
from concourse.masks import make_identity

M, D, E, N, C = 1024, 1024, 512, 2048, 512
FLOPS = 2 * M * N * (D + E) + 2 * M * N * C

F32 = mybir.dt.float32
BF16 = mybir.dt.bfloat16
I32 = mybir.dt.int32
U32 = mybir.dt.uint32
U8 = mybir.dt.uint8
FP8 = mybir.dt.float8_e4m3fn
FP8X4 = mybir.dt.float8_e4m3fn_x4
FP4X4 = mybir.dt.float4_e2m1fn_x4
ALU = mybir.AluOpType
ACT = mybir.ActivationFunctionType

P = 128
K_GROUP = 512
CHUNK = 512
ROW_TILES = M // P
UNITS = 2 * ROW_TILES
LAST_TILE = ROW_TILES - 1
LAST_UNIT = UNITS - 1

G1_BANKS, G2_BANKS = 2, 2
OTHER_BANKS = 4

MANTISSA = 0x007F007F
EXPONENT_OF_ONE = 0x3F803F80
SIGN_AND_EXPONENT = -0x007F0080


def tile_gp_product_kernel_mean_f7_kernel(
    tc, x1_bytes, x1_scale, x2, z1_words, z1_scales, z2_words, z2_scales,
    alpha_words, alpha_scales, lx, lz, amp, gain, prior, out,
):
    nc = tc.nc
    with ExitStack() as ctx:
        keep = ctx.enter_context(tc.tile_pool(name="keep", bufs=1))
        work = ctx.enter_context(tc.tile_pool(name="work", bufs=3))
        psum = ctx.enter_context(tc.psum_pool(name="psum", bufs=1))
        ctx.enter_context(tc.manual_schedule())

        amp_words = keep.tile([P, 16], BF16, name="amp_words")
        amp_rows = keep.tile([P, 16], BF16, name="amp_rows")
        lz_rows = keep.tile([P, 16], BF16, name="lz_rows")
        lx_cols = keep.tile([P, ROW_TILES], BF16, name="lx_cols")
        x1_codes = keep.tile([P, ROW_TILES, D], U8, name="x1_codes", align_bytes=64)
        x2_rows = keep.tile([P, ROW_TILES, E], BF16, name="x2_rows", align_bytes=64)
        z_words = keep.tile([P, 3, 2 * N], U8, name="z_words", align_bytes=256)
        z_planes = keep.tile([P, 3, N], U8, name="z_planes", align_bytes=256)
        a_words = keep.tile([P, 4, 4 * C], U8, name="a_words", align_bytes=256)
        a_planes = keep.tile([P, 4, C], U8, name="a_planes", align_bytes=256)
        gain_all = keep.tile([P, C], BF16, name="gain_all")
        prior_all = keep.tile([P, C], BF16, name="prior_all")
        ident = keep.tile([P, P], F32, name="ident")
        one = keep.tile([P, 1], F32, name="one")
        table_out = keep.tile([P, 2], F32, name="table_out")
        scale_all = keep.tile([P, D], F32, name="scale_all", align_bytes=64)
        mantissa = keep.tile([P, 16], BF16, name="mantissa")
        sigma = keep.tile([P, 16], BF16, name="sigma")
        ln_m = keep.tile([P, 16], F32, name="ln_m")
        shift = keep.tile([P, 16], F32, name="shift")
        scale_cols = keep.tile([P, 2, 4], F32, name="scale_cols")
        minus_lx = keep.tile([P, ROW_TILES], F32, name="minus_lx")
        minus_half_lx = keep.tile([P, ROW_TILES], F32, name="minus_half_lx")
        shift_all = keep.tile([P, N], F32, name="shift_all", align_bytes=64)

        x1_view = x1_bytes.rearrange("(p r) k -> p r k", r=ROW_TILES)
        x2_view = x2.rearrange("(p r) k -> p r k", r=ROW_TILES)
        out_view = out.rearrange("(p r) c -> p r c", r=ROW_TILES)
        z1_view = z1_words.rearrange("g p n -> p g n")
        z2_view = z2_words.rearrange("g p n -> p g n")
        a_view = alpha_words.rearrange("g p n t -> p g (n t)")

        nc.vector.memset(z_planes[:].rearrange("p g n -> p (g n)").bitcast(I32), 0)
        nc.vector.memset(one[:], 1.0)
        make_identity(nc, ident[:])
        nc.gpsimd.memset(a_planes[:].rearrange("p g n -> p (g n)").bitcast(I32), 0)

        def load_x1(first, end):
            nc.sync.dma_start(out=x1_codes[:, first:end, :], in_=x1_view[:, first:end, :])

        def load_x2(first, end):
            nc.sync.dma_start(out=x2_rows[:, first:end, :], in_=x2_view[:, first:end, :])

        def load_scale_bytes(planes, first_group, source):
            groups = source.shape[0]
            for q in range(4):
                nc.sync.dma_start(
                    out=planes[32 * q : 32 * q + 4, first_group : first_group + groups, :].bitcast(I32),
                    in_=source[:, 4 * q : 4 * q + 4, :].rearrange("g q n -> q g n").bitcast(I32),
                )

        def load_z(chunk):
            cols = slice(2 * CHUNK * chunk, 2 * CHUNK * (chunk + 1))
            nc.sync.dma_start(out=z_words[:, 0:2, cols], in_=z1_view[:, :, cols])
            nc.sync.dma_start(out=z_words[:, 2:3, cols], in_=z2_view[:, :, cols])

        nc.scalar.dma_start(out=scale_cols[:], in_=x1_scale.rearrange("o (g p v) -> p (o g) v", g=2, v=4))
        nc.scalar.dma_start(out=amp_rows[:], in_=amp.rearrange("(p v) -> p v", v=16))
        nc.scalar.dma_start(out=lz_rows[:], in_=lz.rearrange("(p v) -> p v", v=16))
        nc.scalar.dma_start(out=lx_cols[:], in_=lx.rearrange("(p r) -> p r", r=ROW_TILES))
        load_x1(0, 1)
        load_x2(0, 1)
        load_x1(1, 3)
        load_scale_bytes(z_planes, 0, z1_scales)
        load_scale_bytes(z_planes, 2, z2_scales)
        load_z(0)
        load_x2(1, 2)
        load_z(1)
        load_z(2)
        load_z(3)
        load_x2(2, 4)
        nc.sync.dma_start(
            out=amp_words[:].rearrange("p (g t) -> p g t", t=4), in_=amp.rearrange("(g p t) -> p g t", p=P, t=4)
        )
        load_x1(3, 5)
        load_scale_bytes(a_planes, 0, alpha_scales)
        nc.sync.dma_start(out=a_words[:], in_=a_view)
        load_x2(4, 8)
        load_x1(5, 8)
        nc.sync.dma_start(out=gain_all[:], in_=gain.partition_broadcast(P))
        nc.sync.dma_start(out=prior_all[:], in_=prior.partition_broadcast(P))

        tiles = {}

        def x_scale(n):
            x1_rows = work.tile([P, D], BF16, name="x1_rows", tag="x1_rows", bufs=6, align_bytes=64)
            for k in (slice(0, 512), slice(512, 1024)) if n == 0 else (slice(0, 1024),):
                nc.vector.tensor_tensor(
                    out=x1_rows[:, k], in0=x1_codes[:, n // 2, k].bitcast(FP8), in1=scale_all[:, k], op=ALU.mult
                )
            tiles["x1_rows", n] = x1_rows

        def x_turn(n):
            x1_pairs = tiles["x1_rows", n][:].bitcast(F32)
            x2_pairs = x2_rows[:, n // 2, :].bitcast(F32)
            x1_turned = psum.tile([P, 4, P], F32, name="x1_turned", tag="other", bufs=OTHER_BANKS)
            x2_turned = psum.tile([P, 4, P], F32, name="x2_turned", tag="other", bufs=OTHER_BANKS)
            for g in range(2):
                for u in range(2):
                    nc.tensor.transpose(
                        x1_turned[:, 2 * g + u, :], x1_pairs[:, 256 * g + u : 256 * (g + 1) : 2], ident[:]
                    )
            for u in range(2):
                nc.tensor.transpose(x2_turned[:, u, :], x2_pairs[:, u:256:2], ident[:])
            tiles["x_turned", n] = (x1_turned, x2_turned)

        def x_copy(n):
            x_grouped = work.tile([P, 3 * K_GROUP], BF16, name="x_grouped", tag="x_grouped", bufs=3, align_bytes=64)
            x1_turned, x2_turned = tiles["x_turned", n]
            pairs = x_grouped[:].bitcast(F32).rearrange("p (g i u) -> p g i u", g=3, u=2)
            for first, end in ((0, 1), (1, 2)) if n == 0 else ((0, 2),):
                nc.scalar.copy(
                    out=pairs[:, first:end],
                    in_=x1_turned[:, 2 * first : 2 * end, :].rearrange("p (g u) i -> p g i u", u=2),
                )
            nc.scalar.copy(out=pairs[:, 2], in_=x2_turned[:, 0:2, :].rearrange("p u i -> p i u"))
            tiles["x_grouped", n] = x_grouped

        def x_quant(n):
            x_words = work.tile([P, 3 * P], U32, name="x_words", tag="x_words", bufs=4, align_bytes=64)
            x_planes = work.tile([P, 3 * P], U8, name="x_planes", tag="x_planes", bufs=4, align_bytes=64)
            for first, end in ((0, 1), (1, 2), (2, 3)) if n == 0 else ((0, 2), (2, 3)):
                nc.vector.quantize_mx(
                    out=x_words[:, P * first : P * end].bitcast(FP8X4),
                    scales=x_planes[:, P * first : P * end],
                    in_=tiles["x_grouped", n][:, K_GROUP * first : K_GROUP * end],
                )
            tiles["x_mx", n // 2] = (x_words, x_planes)

        def x_times_z(acc, n, g, h, start, stop):
            x_words, x_planes = tiles["x_mx", n // 2]
            chunk = 2 * (n % 2) + h
            nc.tensor.matmul_mx(
                out=acc[:],
                lhsT=x_words[:, P * g : P * (g + 1)].bitcast(FP8X4),
                lhsT_scale=x_planes[:, P * g : P * (g + 1)],
                rhs=z_words[:, g, 2 * CHUNK * chunk : 2 * CHUNK * (chunk + 1)].bitcast(FP4X4),
                rhs_scale=z_planes[:, g, CHUNK * chunk : CHUNK * (chunk + 1)],
                start=start,
                stop=stop,
            )

        def g1_mm(n, h):
            acc = psum.tile([P, CHUNK], F32, name="g1", tag="g1", bufs=G1_BANKS)
            x_times_z(acc, n, 0, h, True, False)
            x_times_z(acc, n, 1, h, False, True)
            tiles["g1", n, h] = acc

        def g2_mm(n, h):
            acc = psum.tile([P, CHUNK], F32, name="g2", tag="g2", bufs=G2_BANKS)
            x_times_z(acc, n, 2, h, True, True)
            tiles["g2", n, h] = acc

        def on_gpsimd(n, h):
            return h == 1 and n < LAST_UNIT

        def exponent(n, h):
            chunk = 2 * (n % 2) + h
            t = work.tile([P, CHUNK], F32, name="t", tag="t", bufs=6)
            nc.vector.tensor_tensor(
                out=t[:], in0=tiles["g1", n, h][:], in1=shift_all[:, CHUNK * chunk : CHUNK * (chunk + 1)], op=ALU.subtract
            )
            tiles["t", n, h] = t

        def exponential(n, h):
            r = n // 2
            e = work.tile([P, CHUNK], F32, name="e", tag="e", bufs=8)
            if on_gpsimd(n, h):
                nc.scalar.activation(
                    out=e[:], in_=tiles["t", n, h][:], func=ACT.Exp, bias=minus_lx[:, r : r + 1], scale=1.0
                )
            else:
                nc.scalar.activation(
                    out=e[:], in_=tiles["t", n, h][:], func=ACT.Exp, bias=minus_half_lx[:, r : r + 1], scale=0.5
                )
            tiles["e", n, h] = e

        def poly_square(n, h):
            if on_gpsimd(n, h):
                q = work.tile([P, CHUNK], F32, name="q", tag="q", bufs=5)
                nc.scalar.activation(out=q[:], in_=tiles["g2", n, h][:], func=ACT.Square, bias=1.0, scale=1.0)
                tiles["q", n, h] = q

        def gpsimd_product(n, h):
            if on_gpsimd(n, h):
                c_rows = work.tile([P, CHUNK], BF16, name="c_rows", tag="c_rows", bufs=8, align_bytes=64)
                nc.gpsimd.tensor_tensor(out=c_rows[:], in0=tiles["e", n, h][:], in1=tiles["q", n, h][:], op=ALU.mult)
                tiles["c_rows", n, h] = c_rows

        def root_product(n, h):
            if not on_gpsimd(n, h):
                y = work.tile([P, CHUNK], F32, name="y", tag="y", bufs=4)
                nc.vector.scalar_tensor_tensor(
                    out=y[:], in0=tiles["g2", n, h][:], scalar=1.0, in1=tiles["e", n, h][:], op0=ALU.add, op1=ALU.mult
                )
                tiles["y", n, h] = y

        def root_square(n, h):
            if not on_gpsimd(n, h):
                c_rows = work.tile([P, CHUNK], BF16, name="c_rows", tag="c_rows", bufs=8, align_bytes=64)
                nc.scalar.activation(
                    out=c_rows[:].rearrange("i (u p e) -> i u p e", u=2, e=2),
                    in_=tiles["y", n, h][:].rearrange("i (p u e) -> i u p e", u=2, e=2),
                    func=ACT.Square,
                )
                tiles["c_rows", n, h] = c_rows

        def chunks_now(n, h):
            if n == LAST_UNIT:
                return (h,)
            return (0, 1) if h == 1 else ()

        def c_turn(n, h):
            chunks = chunks_now(n, h)
            if not chunks:
                return
            turned = psum.tile([P, 2, 2, P], F32, name="c_turned", tag="other", bufs=OTHER_BANKS)
            for k in chunks:
                pairs = tiles["c_rows", n, k][:].bitcast(F32)
                for u in range(2):
                    words = pairs[:, u:256:2] if on_gpsimd(n, k) else pairs[:, P * u : P * (u + 1)]
                    nc.tensor.transpose(turned[:, u, k, :], words, ident[:])
                tiles["c_turned", n, k] = turned

        def c_copy(n, h):
            chunks = chunks_now(n, h)
            if not chunks:
                return
            if chunks[0] == 0:
                grouped = work.tile([P, 2 * CHUNK], BF16, name="c_grouped", tag="c_grouped", bufs=4, align_bytes=64)
                tiles["c_grouped", n] = grouped
            first, end = chunks[0], chunks[-1] + 1
            turned = tiles["c_turned", n, h][:, :, first:end, :].bitcast(BF16)
            sigma_cols = sigma[:, 8 * (n % 2) + 4 * first : 8 * (n % 2) + 4 * end].rearrange(
                "p (c o u e) -> p c o u e", o=1, u=2, e=2
            )
            nc.vector.tensor_tensor(
                out=tiles["c_grouped", n][:, CHUNK * first : CHUNK * end].rearrange(
                    "p (c i u e) -> p c i u e", i=P, u=2, e=2
                ),
                in0=turned.rearrange("p u c (i e) -> p c i u e", e=2),
                in1=sigma_cols.to_broadcast([P, end - first, P, 2, 2]),
                op=ALU.mult,
            )

        def c_quant(n, h):
            chunks = chunks_now(n, h)
            if not chunks:
                return
            if chunks[0] == 0:
                words = work.tile([P, 2 * P], U32, name="c_words", tag="c_words", bufs=4, align_bytes=64)
                planes = work.tile([P, 2 * P], U8, name="c_planes", tag="c_planes", bufs=4, align_bytes=64)
                tiles["c_mx", n] = (words, planes)
            c_words, c_planes = tiles["c_mx", n]
            first, end = chunks[0], chunks[-1] + 1
            nc.vector.quantize_mx(
                out=c_words[:, P * first : P * end].bitcast(FP8X4),
                scales=c_planes[:, P * first : P * end],
                in_=tiles["c_grouped", n][:, CHUNK * first : CHUNK * end],
            )

        def c_times_a(acc, r, chunk):
            c_words, c_planes = tiles["c_mx", 2 * r + chunk // 2]
            cols = slice(P * (chunk % 2), P * (chunk % 2 + 1))
            nc.tensor.matmul_mx(
                out=acc[:],
                lhsT=c_words[:, cols].bitcast(FP8X4),
                lhsT_scale=c_planes[:, cols],
                rhs=a_words[:, chunk, :].bitcast(FP8X4),
                rhs_scale=a_planes[:, chunk, :],
                start=(chunk == 0),
                stop=(chunk == 3),
            )

        def f_mm(n, h):
            r = n // 2
            chunk = 2 * (n % 2) + h
            passes = (chunk,) if r == LAST_TILE else range(4) if chunk == 3 else ()
            for c in passes:
                if c == 0:
                    acc = psum.tile([P, C], F32, name="f", tag="other", bufs=OTHER_BANKS)
                    tiles["f", r] = acc
                c_times_a(tiles["f", r], r, c)

        output_halves = (slice(0, C // 2), slice(C // 2, C))

        def f_gain(n):
            r = n // 2
            if r == LAST_TILE:
                scaled = work.tile([P, C], F32, name="scaled_last", tag="scaled_last", bufs=1)
                for c in output_halves:
                    nc.vector.tensor_tensor(out=scaled[:, c], in0=tiles["f", r][:, c], in1=gain_all[:, c], op=ALU.mult)
            else:
                scaled = work.tile([P, C], F32, name="scaled", tag="scaled", bufs=2)
                nc.vector.tensor_tensor(out=scaled[:], in0=tiles["f", r][:], in1=gain_all[:], op=ALU.mult)
            tiles["scaled", r] = scaled

        def f_prior(n):
            r = n // 2
            mean = work.tile([P, C], F32, name="mean", tag="mean", bufs=3)
            scaled = tiles["scaled", r]
            if r < LAST_TILE - 1:
                nc.gpsimd.tensor_tensor(out=mean[:], in0=scaled[:], in1=prior_all[:], op=ALU.add)
                nc.sync.dma_start(out=out_view[:, r, :], in_=mean[:])
            elif r < LAST_TILE:
                nc.vector.tensor_tensor(out=mean[:], in0=scaled[:], in1=prior_all[:], op=ALU.add)
                nc.sync.dma_start(out=out_view[:, r, :], in_=mean[:])
            else:
                for c in output_halves:
                    nc.vector.tensor_tensor(out=mean[:, c], in0=scaled[:, c], in1=prior_all[:, c], op=ALU.add)
                    nc.sync.dma_start(out=out_view[:, r, c], in_=mean[:, c])

        def make_ln():
            nc.scalar.activation(out=table_out[:, 0:1], in_=one[:], func=ACT.Ln)
            nc.vector.tensor_scalar(
                out=mantissa[:].bitcast(I32), in0=amp_rows[:].bitcast(I32), scalar1=MANTISSA,
                scalar2=EXPONENT_OF_ONE, op0=ALU.bitwise_and, op1=ALU.bitwise_or,
            )
            nc.scalar.activation(out=ln_m[:], in_=mantissa[:], func=ACT.Ln)

        def make_shift():
            nc.vector.tensor_tensor(out=shift[:], in0=lz_rows[:], in1=ln_m[:], op=ALU.subtract)

        def load_exp_table():
            nc.scalar.activation(out=table_out[:, 1:2], in_=one[:], func=ACT.Exp)

        def spread_scale():
            banks = []
            for g in range(2):
                spread = psum.tile([P, 4, P], F32, name="scale_spread", tag="g1", bufs=G1_BANKS)
                banks.append(spread)
            for g in range(2):
                for v in range(4):
                    nc.tensor.transpose(banks[g][:, v, :], scale_cols[:, g, v : v + 1].to_broadcast([P, P]), ident[:])
                cols = scale_all[:, K_GROUP * g : K_GROUP * (g + 1)].rearrange("i (p v) -> i p v", v=4)
                if g == 0:
                    nc.vector.tensor_copy(out=cols, in_=banks[g][:].rearrange("i v p -> i p v"))
                else:
                    nc.scalar.copy(out=cols, in_=banks[g][:].rearrange("i v p -> i p v"))

        def make_lx():
            nc.vector.tensor_scalar(out=minus_lx[:], in0=lx_cols[:], scalar1=-1.0, scalar2=None, op0=ALU.mult)
            nc.vector.tensor_scalar(out=minus_half_lx[:], in0=lx_cols[:], scalar1=-0.5, scalar2=None, op0=ALU.mult)

        def spread_shift(quarter):
            spread = psum.tile([P, 4, P], F32, name="shift_spread", tag="g2", bufs=G2_BANKS)
            for k in range(4):
                v = 4 * quarter + k
                nc.tensor.transpose(spread[:, k, :], shift[:, v : v + 1].to_broadcast([P, P]), ident[:])
            nc.scalar.copy(
                out=shift_all[:].rearrange("i (p v) -> i p v", v=16)[:, :, 4 * quarter : 4 * quarter + 4],
                in_=spread[:].rearrange("i k p -> i p k"),
            )

        def make_sigma():
            nc.vector.tensor_scalar(
                out=sigma[:].bitcast(I32), in0=amp_words[:].bitcast(I32), scalar1=SIGN_AND_EXPONENT,
                scalar2=None, op0=ALU.bitwise_and,
            )

        stages = (
            (c_turn, 3, 0),
            (g1_mm, 0, 1),
            (c_quant, 4, 0),
            (c_turn, 3, 1),
            (root_product, 2, 0),
            (x_quant, -2, None),
            (c_quant, 4, 1),
            (exponential, 1, 1),
            (root_square, 2, 1),
            (x_scale, -5, None),
            (f_gain, 5, None),
            (gpsimd_product, 2, 1),
            (x_turn, -3, None),
            (f_prior, 6, None),
            (poly_square, 1, 1),
            (exponent, 0, 1),
            (g1_mm, -1, 0),
            (exponential, 1, 0),
            (g2_mm, 1, 0),
            (c_copy, 3, 0),
            (root_product, 1, 1),
            (f_mm, 4, 0),
            (root_square, 2, 0),
            (g2_mm, 0, 1),
            (f_mm, 4, 1),
            (c_copy, 3, 1),
            (exponent, -1, 0),
            (x_copy, -3, None),
        )
        x_stages = (x_scale, x_turn, x_copy, x_quant)
        f_stages = (f_gain, f_prior)

        constants = {
            -9: (make_ln,),
            -8: (spread_scale, make_shift, lambda: spread_shift(0)),
            -7: (make_lx,),
            -6: (lambda: spread_shift(1),),
            -2: (lambda: spread_shift(2),),
            -1: (lambda: spread_shift(3),),
            0: (load_exp_table,),
            1: (make_sigma,),
        }

        first_step = min(constants)
        last_step = LAST_UNIT + max([lag for stage, lag, h in stages])
        for s in range(first_step, last_step + 1):
            for make in constants.get(s, ()):
                make()
            for stage, lag, h in stages:
                n = s - lag
                if not 0 <= n <= LAST_UNIT:
                    continue
                if h is not None:
                    stage(n, h)
                elif (stage in x_stages and n % 2 == 0) or (stage in f_stages and n % 2 == 1):
                    stage(n)
